import numpy as np
import ml_dtypes


def mxq(x, axis, fmt="e4m3"):
    dtype, down = {"e4m3": (ml_dtypes.float8_e4m3fn, 7), "e5m2": (ml_dtypes.float8_e5m2, 14)}[fmt]
    v = np.moveaxis(np.asarray(x, np.float32).astype(ml_dtypes.bfloat16).astype(np.float64), axis, -1)
    blocks = v.reshape(v.shape[:-1] + (-1, 32))
    amax = np.abs(blocks).max(-1, keepdims=True)
    byte = np.maximum(np.where(amax > 0, np.frexp(amax)[1] - 1 + 127, 0) - down, 1)
    scale = np.exp2(byte - 127.0)
    codes = (blocks / scale).astype(np.float32).astype(dtype).astype(np.float64)
    return np.moveaxis((codes * scale).reshape(v.shape), -1, axis)


WIDE = False


def mx_kscale(k):
    if not WIDE:
        return np.ones(k)
    levels = np.array([10, -10, 5, -5, 0])
    if k % 512:
        return np.exp2(np.random.permutation(np.resize(levels, k // 32))).repeat(32)
    a = np.empty((k // 512, 16))
    for p in range(k // 512):
        a[p, :8] = np.random.permutation(np.resize(levels, 8))
        for g in range(8):
            far = levels[np.abs(levels - a[p, g]) >= 10]
            a[p, g + 8] = far[np.random.randint(len(far))]
    return np.exp2(a.ravel()).repeat(32)


BF16 = ml_dtypes.bfloat16


def bf(x):
    return np.asarray(x, np.float32).astype(BF16)


def f64(x):
    return np.asarray(x).astype(np.float64)


E2M1 = np.array([0.0, 0.5, 1.0, 1.5, 2.0, 3.0, 4.0, 6.0, -0.0, -0.5, -1.0, -1.5, -2.0, -3.0, -4.0, -6.0])


def pack_weight(w, fmt):
    k, n = w.shape
    w = f64(bf(w)).reshape(k // 32, 32, n)
    amax = np.abs(w).max(1)
    if fmt == "e4m3":
        byte = np.frexp(amax)[1] - 1 + 127 - 7
    else:
        mant, ex = np.frexp(amax / 6.0)
        byte = np.where(mant > 0.5, ex, ex - 1) + 127
    byte = np.clip(np.where(amax > 0, byte, 1), 1, 254)
    scaled = (w * np.exp2(127.0 - byte)[:, None, :]).reshape(k, n).astype(np.float32)
    by_word = np.ascontiguousarray(scaled.reshape(k // 512, 128, 4, n).transpose(0, 1, 3, 2))
    if fmt == "e4m3":
        words = by_word.astype(ml_dtypes.float8_e4m3fn).view(np.uint8)
    else:
        c = by_word.astype(ml_dtypes.float4_e2m1fn).view(np.uint8) & 0xF
        words = c[..., 0::2] | (c[..., 1::2] << 4)
    return np.ascontiguousarray(words), np.ascontiguousarray(byte.astype(np.uint8).reshape(k // 512, 16, n))


def unpack_weight(words, scales, fmt):
    g, p, n, _ = words.shape
    if fmt == "e4m3":
        vals = np.ascontiguousarray(words).view(ml_dtypes.float8_e4m3fn).astype(np.float64)
    else:
        nib = np.empty((g, p, n, 4), np.uint8)
        nib[..., 0::2] = words & 0xF
        nib[..., 1::2] = words >> 4
        vals = E2M1[nib]
    vals = vals * np.repeat(np.exp2(scales.astype(np.float64) - 127.0), 8, axis=1)[..., None]
    return vals.transpose(0, 1, 3, 2).reshape(g * 512, n)
def pack4(w):
    words, scales = pack_weight(w, "e2m1")
    return words.reshape(words.shape[0], 128, -1), scales


def unpack4(words, scales):
    return unpack_weight(words.reshape(words.shape[0], 128, -1, 2), scales, "e2m1")


def planes(Y):
    n, m = Y.shape
    b = f64(bf(Y)).reshape(n // 32, 32, m)
    amax = np.abs(b).max(1)
    byte = np.clip(np.where(amax > 0, np.frexp(amax)[1] - 1 + 127 - 7, 1), 1, 254)
    codes = (b * np.exp2(127.0 - byte)[:, None, :]).reshape(n, m).astype(np.float32).astype(ml_dtypes.float8_e4m3fn).view(np.uint8)
    words = codes.reshape(n // 512, 128, 4, m).transpose(0, 1, 3, 2)
    return np.ascontiguousarray(words), np.ascontiguousarray(byte.astype(np.uint8).reshape(n // 512, 16, m))


R, K1, K2, D, P = 1024, 512, 1024, 1536, 1024

def setup_inputs():
    randn = np.random.randn
    s1, s2, t = mx_kscale(K1), mx_kscale(K2), mx_kscale(D)
    coef_lead = bf(randn(R, K1) * s1)
    basis_lead = bf(0.5 * randn(K1, D) / np.sqrt(K1) / s1[:, None])
    coef_fine = bf(randn(R, K2) * s2)
    fine_words, fine_scales = pack4(0.35 * randn(K2, D) / np.sqrt(K2) / s2[:, None])
    cos_weight = bf((0.1 + 0.9 * np.random.rand(D)) * t)
    light_words, light_scales = pack_weight(randn(D, P) / np.sqrt(D) / t[:, None], "e4m3")
    tint = bf(1 + 0.1 * randn(R))
    bounce = bf(0.4 * randn(R, P))
    power = bf(np.exp(0.8 * randn(P)))
    return dict(coef_lead=coef_lead, basis_lead=basis_lead, coef_fine=coef_fine, fine_words=fine_words,
                fine_scales=fine_scales, cos_weight=cos_weight, light_words=light_words,
                light_scales=light_scales, tint=tint, bounce=bounce, power=power)

def reference(coef_lead, basis_lead, coef_fine, fine_words, fine_scales, cos_weight, light_words, light_scales, tint, bounce, power):
    lead = mxq(f64(coef_lead), 1, "e4m3") @ mxq(f64(basis_lead), 0, "e4m3")
    fine = mxq(f64(coef_fine), 1, "e4m3") @ unpack4(fine_words, fine_scales)
    F = np.exp(lead + fine) * f64(cos_weight)
    acc = mxq(F, 1, "e4m3") @ unpack_weight(light_words, light_scales, "e4m3")
    y = (acc * f64(tint)[:, None] + f64(bounce)) * f64(power)
    Y = y.T
    words, scales = planes(Y)
    return y, words, scales

@@ -1,0 +1,415 @@
+from contextlib import ExitStack
+
+import concourse.mybir as mybir
+from concourse.masks import make_identity
+
+R, K1, K2, D, NL = 1024, 512, 1024, 1536, 1024
+FLOPS = 2 * R * (K1 + K2) * D + 2 * R * D * NL
+
+F32 = mybir.dt.float32
+BF16 = mybir.dt.bfloat16
+I32 = mybir.dt.int32
+U32 = mybir.dt.uint32
+U8 = mybir.dt.uint8
+FP8X4 = mybir.dt.float8_e4m3fn_x4
+FP4X4 = mybir.dt.float4_e2m1fn_x4
+ACT = mybir.ActivationFunctionType
+ALU = mybir.AluOpType
+
+P = 128
+KP = 512
+
+
+def tile_log_brdf_environment_transport_k6_kernel(
+    tc, coef_lead, basis_lead, coef_fine, fine_words, fine_scales, cos_weight,
+    light_words, light_scales, tint, bounce, power, out_0, out_1, out_2,
+):
+    nc = tc.nc
+    with ExitStack() as ctx:
+        keep = ctx.enter_context(tc.tile_pool(name="keep", bufs=1))
+        work = ctx.enter_context(tc.tile_pool(name="work", bufs=1))
+        psum = ctx.enter_context(tc.psum_pool(name="psum", bufs=8))
+        ctx.enter_context(tc.manual_schedule())
+
+        def kept(name, shape, dtype):
+            return keep.tile(shape, dtype, name=name, align_bytes=64)
+
+        def bank(shape):
+            return psum.tile(shape, F32, name="bank")
+
+        ident = kept("ident", [P, P], F32)
+        warm = kept("warm", [P, 16], F32)
+        fine_scale_raw = kept("fine_scale_raw", [P, 2, D], U8)
+        light_scale = kept("light_scale", [P, 3, NL], U8)
+        cos_sb = kept("cos_sb", [P, 3, 4], BF16)
+        tint_sb = kept("tint_sb", [P, 4, 2], BF16)
+        power_sb = kept("power_sb", [P, NL], BF16)
+        y_scale = kept("y_scale", [P, 2, R], U8)
+
+        make_identity(nc, ident[:])
+        nc.vector.memset(fine_scale_raw[:].bitcast(I32), 0)
+        nc.vector.memset(warm[:], 0.0)
+        nc.vector.memset(light_scale[:].bitcast(I32), 0)
+        nc.scalar.activation(out=warm[:, 8:9], in_=warm[:, 0:1], func=ACT.Exp)
+
+        lead_raw, fine_coef_raw, basis_raw, fine_raw, light, bounce_sb = {}, {}, {}, {}, {}, {}
+
+        def load_lead(h):
+            lead_raw[h] = kept("lead_raw_%d" % h, [P, 2, 2 * K1], BF16)
+            nc.sync.dma_start(
+                out=lead_raw[h][:],
+                in_=coef_lead[512 * h : 512 * (h + 1), :].rearrange("(q p i) k -> p q (i k)", q=2, i=2),
+            )
+
+        def load_fine(q):
+            fine_coef_raw[q] = kept("fine_coef_raw_%d" % q, [P, 2 * K2], BF16)
+            nc.sync.dma_start(
+                out=fine_coef_raw[q][:],
+                in_=coef_fine[256 * q : 256 * (q + 1), :].rearrange("(p i) k -> p (i k)", i=2),
+            )
+
+        def load_words(g):
+            fine_raw[g] = kept("fine_raw_%d" % g, [P, 2, 2 * KP], U8)
+            nc.sync.dma_start(
+                out=fine_raw[g][:].bitcast(I32),
+                in_=fine_words[:, :, 2 * KP * g : 2 * KP * (g + 1)].rearrange("k p b -> p k b").bitcast(I32),
+            )
+
+        def load_basis(g):
+            basis_raw[g] = kept("basis_raw_%d" % g, [P, 4, KP], BF16)
+            nc.sync.dma_start(
+                out=basis_raw[g][:],
+                in_=basis_lead[:, KP * g : KP * (g + 1)].rearrange("(p j) d -> p j d", j=4),
+            )
+
+        load_lead(0)
+        for quad in range(4):
+            nc.sync.dma_start(
+                out=fine_scale_raw[32 * quad : 32 * quad + 4, :, :].bitcast(I32),
+                in_=fine_scales[:, 4 * quad : 4 * quad + 4, :].rearrange("k r n -> r k n").bitcast(I32),
+            )
+        load_words(0)
+        load_basis(0)
+        load_fine(0)
+        load_fine(1)
+        load_words(1)
+        load_basis(1)
+        nc.sync.dma_start(out=cos_sb[:], in_=cos_weight.rearrange("(g p t) -> p g t", g=3, t=4))
+        load_words(2)
+        load_basis(2)
+        load_lead(1)
+        load_fine(2)
+        load_fine(3)
+        for quad in range(4):
+            nc.sync.dma_start(
+                out=light_scale[32 * quad : 32 * quad + 4, :, :].bitcast(I32),
+                in_=light_scales[:, 4 * quad : 4 * quad + 4, :].rearrange("g r n -> r g n").bitcast(I32),
+            )
+        for g in range(3):
+            light[g] = kept("light_%d" % g, [P, NL], U32)
+            nc.sync.dma_start(
+                out=light[g][:].bitcast(I32),
+                in_=light_words[g].rearrange("p n t -> p (n t)").bitcast(I32),
+            )
+        nc.sync.dma_start(out=tint_sb[:], in_=tint.rearrange("(q p i) -> p q i", q=4, i=2))
+        nc.sync.dma_start(out=power_sb[:], in_=power.partition_broadcast(P))
+        for q in range(4):
+            bounce_sb[q] = kept("bounce_%d" % q, [P, 2, NL], BF16)
+            nc.sync.dma_start(
+                out=bounce_sb[q][:],
+                in_=bounce[256 * q : 256 * (q + 1), :].rearrange("(p i) n -> p i n", i=2),
+            )
+
+        coef_grouped, coef_code, coef_scale = {}, {}, {}
+
+        def turn_coef(c, q):
+            turned = bank([P, 2, 2, P])
+            for i in range(2):
+                if c == 0:
+                    words = lead_raw[q // 2][:, q % 2, :].bitcast(F32)[:, 256 * i : 256 * (i + 1)]
+                else:
+                    first = 512 * i + 256 * (c - 1)
+                    words = fine_coef_raw[q][:].bitcast(F32)[:, first : first + 256]
+                for u in range(2):
+                    nc.tensor.transpose(turned[:, i, u, :], words[:, u:256:2], ident[:])
+            coef_grouped[c, q] = work.tile([P, 1024], BF16, name="coef_grouped", bufs=6, align_bytes=64)
+            nc.scalar.copy(
+                out=coef_grouped[c, q][:].bitcast(F32).rearrange("p (i r u) -> p i r u", i=2, u=2),
+                in_=turned[:].rearrange("p i u r -> p i r u"),
+            )
+
+        def quantize_coef(c, q):
+            h = q // 2
+            if q % 2 == 0:
+                coef_code[c, h] = kept("coef_code_%d_%d" % (c, h), [P, 512], U32)
+                coef_scale[c, h] = kept("coef_scale_%d_%d" % (c, h), [P, 512], U8)
+            cols = slice(256 * (q % 2), 256 * (q % 2 + 1))
+            nc.vector.quantize_mx(
+                out=coef_code[c, h][:, cols].bitcast(FP8X4),
+                scales=coef_scale[c, h][:, cols],
+                in_=coef_grouped[c, q][:],
+            )
+
+        fine_code, fine_scale, basis_grouped, basis_code, basis_scale = {}, {}, {}, {}, {}
+
+        def order_fine_codes(g):
+            fine_code[g] = kept("fine_code_%d" % g, [P, 4, 2, 2 * P], U8)
+            nc.vector.tensor_copy(
+                out=fine_code[g][:].rearrange("p t k (a m b) -> p (k a) t m b", m=8, b=2),
+                in_=fine_raw[g][:].rearrange("p k (a m t b) -> p (k a) t m b", m=8, t=4, b=2),
+            )
+
+        def order_fine_scales(g):
+            fine_scale[g] = kept("fine_scale_%d" % g, [P, 4, 2, P], U8)
+            nc.vector.tensor_copy(
+                out=fine_scale[g][:].rearrange("p t k (a m) -> p k a t m", m=16),
+                in_=fine_scale_raw[:, :, KP * g : KP * (g + 1)].rearrange("p k (a m t) -> p k a t m", m=16, t=4),
+            )
+
+        def group_basis(g, copy, part, parts):
+            if part == 0:
+                basis_grouped[g] = kept("basis_grouped_%d" % g, [P, 4, P, 4], BF16)
+            a = slice(part * 64 // parts, (part + 1) * 64 // parts)
+            copy(
+                out=basis_grouped[g][:].rearrange("p t (a m) j -> p a t m j", m=2)[:, a],
+                in_=basis_raw[g][:].rearrange("p j (a m t) -> p a t m j", m=2, t=4)[:, a],
+            )
+
+        def quantize_basis(g):
+            basis_code[g] = kept("basis_code_%d" % g, [P, KP], U32)
+            basis_scale[g] = kept("basis_scale_%d" % g, [P, KP], U8)
+            nc.vector.quantize_mx(
+                out=basis_code[g][:].bitcast(FP8X4),
+                scales=basis_scale[g][:],
+                in_=basis_grouped[g][:].rearrange("p t m j -> p (t m j)"),
+            )
+
+        log_brdf, brdf, f_grouped, f_code, f_scale = {}, {}, {}, {}, {}
+
+        def stage1_pass(g, h, t, c):
+            if c == 0:
+                log_brdf[g, h, t] = bank([P, 512])
+                weights = basis_code[g][:, P * t : P * (t + 1)].bitcast(FP8X4)
+                scales = basis_scale[g][:, P * t : P * (t + 1)]
+            else:
+                weights = fine_code[g][:, t, c - 1, :].bitcast(FP4X4)
+                scales = fine_scale[g][:, t, c - 1, :]
+            nc.tensor.matmul_mx(
+                out=log_brdf[g, h, t][:], lhsT=weights, lhsT_scale=scales,
+                rhs=coef_code[c, h][:].bitcast(FP8X4), rhs_scale=coef_scale[c, h][:],
+                start=(c == 0), stop=(c == 2),
+            )
+
+        def exponentiate(g, h, t):
+            if t == 0:
+                brdf[g, h] = work.tile([P, 4, 512], F32, name="brdf", bufs=3)
+            nc.scalar.activation(out=brdf[g, h][:, t, :], in_=log_brdf[g, h, t][:], func=ACT.Exp)
+
+        def weigh(g, h):
+            f_grouped[g, h] = work.tile([P, 2048], BF16, name="f_grouped", bufs=2, align_bytes=64)
+            nc.vector.tensor_tensor(
+                out=f_grouped[g, h][:].rearrange("p (a r t) -> p a t r", r=4, t=4),
+                in0=brdf[g, h][:].rearrange("p t (a r) -> p a t r", r=4),
+                in1=cos_sb[:, g, :].rearrange("p (a t r) -> p a t r", a=1, r=1).to_broadcast([P, 128, 4, 4]),
+                op=ALU.mult,
+            )
+
+        def quantize_f(g, h):
+            f_code[g, h] = kept("f_code_%d_%d" % (g, h), [P, 512], U32)
+            f_scale[g, h] = kept("f_scale_%d_%d" % (g, h), [P, 512], U8)
+            nc.vector.quantize_mx(
+                out=f_code[g, h][:].bitcast(FP8X4), scales=f_scale[g, h][:], in_=f_grouped[g, h][:]
+            )
+
+        lit, y_sorted, y_grouped, y_code, accs = {}, {}, {}, {}, {}
+
+        def stage2_pass(k, half, g):
+            h = k // 4
+            cols = slice(P * (k % 4), P * (k % 4 + 1))
+            n = slice(512 * half, 512 * (half + 1))
+            if g == 0:
+                accs[k, half] = bank([P, 512])
+            nc.tensor.matmul_mx(
+                out=accs[k, half][:], lhsT=f_code[g, h][:, cols].bitcast(FP8X4), lhsT_scale=f_scale[g, h][:, cols],
+                rhs=light[g][:, n].bitcast(FP8X4), rhs_scale=light_scale[:, g, n],
+                start=(g == 0), stop=(g == 2),
+            )
+
+        def tint_rows(k, half):
+            q, i = divmod(k, 2)
+            n = slice(512 * half, 512 * (half + 1))
+            lit[k, half] = work.tile([P, 512], F32, name="lit", bufs=4)
+            nc.vector.scalar_tensor_tensor(
+                out=lit[k, half][:], in0=accs[k, half][:], scalar=tint_sb[:, q, i : i + 1],
+                in1=bounce_sb[q][:, i, n], op0=ALU.mult, op1=ALU.add,
+            )
+
+        def stage2(k):
+            for half in range(2):
+                for g in range(3):
+                    stage2_pass(k, half, g)
+
+        def finish_rows(k, half):
+            q, i = divmod(k, 2)
+            n = slice(512 * half, 512 * (half + 1))
+            y = work.tile([P, 512], F32, name="y", bufs=6)
+            nc.vector.tensor_tensor(out=y[:], in0=lit[k, half][:], in1=power_sb[:, n], op=ALU.mult)
+            nc.sync.dma_start(
+                out=out_0[256 * q : 256 * (q + 1), n].rearrange("(p i) n -> p i n", i=2)[:, i, :], in_=y[:]
+            )
+            y_sorted[k, half] = work.tile([P, 512], BF16, name="y_sorted", bufs=8)
+            nc.scalar.copy(
+                out=y_sorted[k, half][:].rearrange("p (u j e) -> p u j e", u=2, e=2),
+                in_=y[:].rearrange("p (j u e) -> p u j e", u=2, e=2),
+            )
+
+        def epilogue(k):
+            tint_rows(k, 0)
+            tint_rows(k, 1)
+            finish_rows(k, 0)
+            finish_rows(k, 1)
+
+        def turn_y(q, g):
+            turned = bank([P, 2, 2, P])
+            for i in range(2):
+                words = y_sorted[2 * q + i, g][:].bitcast(F32)
+                for u in range(2):
+                    nc.tensor.transpose(turned[:, i, u, :], words[:, P * u : P * (u + 1)], ident[:])
+            y_grouped[q, g] = work.tile([P, 1024], BF16, name="y_grouped", bufs=4, align_bytes=64)
+            nc.scalar.copy(
+                out=y_grouped[q, g][:].bitcast(F32).rearrange("p (r i u) -> p r i u", i=2, u=2),
+                in_=turned[:].rearrange("p i u r -> p r i u"),
+            )
+
+        def quantize_y(q, g):
+            m = slice(256 * q, 256 * (q + 1))
+            y_code[q, g] = kept("y_code_%d_%d" % (q, g), [P, 256], U32)
+            nc.vector.quantize_mx(
+                out=y_code[q, g][:].bitcast(FP8X4), scales=y_scale[:, g, m], in_=y_grouped[q, g][:]
+            )
+            nc.sync.dma_start(
+                out=out_1[g, :, m, :].rearrange("p m t -> p (m t)").bitcast(I32), in_=y_code[q, g][:].bitcast(I32)
+            )
+
+        def unit(g, h, beside=None):
+            for t in range(4):
+                for c in range(3):
+                    stage1_pass(g, h, t, c)
+                exponentiate(g, h, t)
+                if beside is not None:
+                    beside(t)
+
+        turn_coef(0, 0)
+        turn_coef(0, 1)
+        order_fine_scales(0)
+        order_fine_codes(0)
+        quantize_coef(0, 0)
+        quantize_coef(0, 1)
+        group_basis(0, nc.vector.tensor_copy, 0, 1)
+        order_fine_scales(1)
+        quantize_basis(0)
+        for q in range(2):
+            for c in (1, 2):
+                turn_coef(c, q)
+        for q in range(2):
+            for c in (1, 2):
+                quantize_coef(c, q)
+        for t in range(4):
+            stage1_pass(0, 0, t, 0)
+        group_basis(1, nc.scalar.copy, 0, 1)
+        order_fine_codes(1)
+        order_fine_scales(2)
+        quantize_basis(1)
+        order_fine_codes(2)
+        for t in range(4):
+            for c in (1, 2):
+                stage1_pass(0, 0, t, c)
+            exponentiate(0, 0, t)
+        turn_coef(0, 2)
+        turn_coef(0, 3)
+        group_basis(2, nc.vector.tensor_copy, 0, 1)
+        weigh(0, 0)
+        quantize_basis(2)
+        quantize_coef(0, 2)
+        quantize_coef(0, 3)
+        quantize_f(0, 0)
+        unit(1, 0)
+        for q in (2, 3):
+            for c in (1, 2):
+                turn_coef(c, q)
+        weigh(1, 0)
+        for q in (2, 3):
+            for c in (1, 2):
+                quantize_coef(c, q)
+        quantize_f(1, 0)
+        unit(2, 0)
+        weigh(2, 0)
+        unit(0, 1)
+        quantize_f(2, 0)
+        stage2(0)
+        weigh(0, 1)
+        unit(1, 1)
+        tint_rows(0, 0)
+        quantize_f(0, 1)
+        tint_rows(0, 1)
+        stage2(1)
+        finish_rows(0, 0)
+        finish_rows(0, 1)
+        weigh(1, 1)
+        stage2(2)
+        tint_rows(1, 0)
+        quantize_f(1, 1)
+        tint_rows(1, 1)
+        unit(2, 1)
+        finish_rows(1, 0)
+        finish_rows(1, 1)
+        tint_rows(2, 0)
+        tint_rows(2, 1)
+        stage2(3)
+        turn_y(0, 0)
+        turn_y(0, 1)
+        weigh(2, 1)
+        finish_rows(2, 0)
+        quantize_f(2, 1)
+        finish_rows(2, 1)
+        for k in (4, 5):
+            for half in range(2):
+                for g in range(3):
+                    stage2_pass(k, half, g)
+        tint_rows(3, 0)
+        tint_rows(3, 1)
+        quantize_y(0, 0)
+        quantize_y(0, 1)
+        finish_rows(3, 0)
+        finish_rows(3, 1)
+        epilogue(4)
+        turn_y(1, 0)
+        turn_y(1, 1)
+        for k in (6, 7):
+            for g in range(3):
+                stage2_pass(k, 0, g)
+        epilogue(5)
+        quantize_y(1, 0)
+        quantize_y(1, 1)
+        for k in (6, 7):
+            for g in range(3):
+                stage2_pass(k, 1, g)
+        turn_y(2, 0)
+        turn_y(2, 1)
+        for half in range(2):
+            tint_rows(6, half)
+            tint_rows(7, half)
+            finish_rows(6, half)
+            finish_rows(7, half)
+            if half == 0:
+                turn_y(3, 0)
+        quantize_y(2, 0)
+        quantize_y(2, 1)
+        quantize_y(3, 0)
+        turn_y(3, 1)
+        quantize_y(3, 1)
+        for quad in range(4):
+            nc.sync.dma_start(
+                out=out_2[:, 4 * quad : 4 * quad + 4, :].rearrange("g r m -> r g m").bitcast(I32),
+                in_=y_scale[32 * quad : 32 * quad + 4, :, :].bitcast(I32),
+            )

@@ -28,14 +28,14 @@ def tile_log_brdf_environment_transport_k6_kernel(
     with ExitStack() as ctx:
         keep = ctx.enter_context(tc.tile_pool(name="keep", bufs=1))
         work = ctx.enter_context(tc.tile_pool(name="work", bufs=1))
-        psum = ctx.enter_context(tc.psum_pool(name="psum", bufs=8))
+        psum = ctx.enter_context(tc.psum_pool(name="psum", bufs=1))
         ctx.enter_context(tc.manual_schedule())
 
         def kept(name, shape, dtype):
             return keep.tile(shape, dtype, name=name, align_bytes=64)
 
         def bank(shape):
-            return psum.tile(shape, F32, name="bank")
+            return psum.tile(shape, F32, name="bank", bufs=8)
 
         ident = kept("ident", [P, P], F32)
         warm = kept("warm", [P, 16], F32)
@@ -94,9 +94,9 @@ def tile_log_brdf_environment_transport_k6_kernel(
         load_fine(1)
         load_words(1)
         load_basis(1)
-        nc.sync.dma_start(out=cos_sb[:], in_=cos_weight.rearrange("(g p t) -> p g t", g=3, t=4))
         load_words(2)
         load_basis(2)
+        nc.sync.dma_start(out=cos_sb[:], in_=cos_weight.rearrange("(g p t) -> p g t", g=3, t=4))
         load_lead(1)
         load_fine(2)
         load_fine(3)
@@ -166,22 +166,20 @@ def tile_log_brdf_environment_transport_k6_kernel(
                 in_=fine_scale_raw[:, :, KP * g : KP * (g + 1)].rearrange("p k (a m t) -> p k a t m", m=16, t=4),
             )
 
-        def group_basis(g, copy, part, parts):
-            if part == 0:
-                basis_grouped[g] = kept("basis_grouped_%d" % g, [P, 4, P, 4], BF16)
-            a = slice(part * 64 // parts, (part + 1) * 64 // parts)
+        def group_basis(g, pair, copy):
+            basis_grouped[g, pair] = kept("basis_grouped_%d_%d" % (g, pair), [P, 2, P, 4], BF16)
             copy(
-                out=basis_grouped[g][:].rearrange("p t (a m) j -> p a t m j", m=2)[:, a],
-                in_=basis_raw[g][:].rearrange("p j (a m t) -> p a t m j", m=2, t=4)[:, a],
+                out=basis_grouped[g, pair][:].rearrange("p t (a m) j -> p a t m j", m=2),
+                in_=basis_raw[g][:].rearrange("p j (a m t) -> p a t m j", m=2, t=4)[:, :, 2 * pair : 2 * pair + 2],
             )
 
-        def quantize_basis(g):
-            basis_code[g] = kept("basis_code_%d" % g, [P, KP], U32)
-            basis_scale[g] = kept("basis_scale_%d" % g, [P, KP], U8)
+        def quantize_basis(g, pair):
+            basis_code[g, pair] = kept("basis_code_%d_%d" % (g, pair), [P, 2 * P], U32)
+            basis_scale[g, pair] = kept("basis_scale_%d_%d" % (g, pair), [P, 2 * P], U8)
             nc.vector.quantize_mx(
-                out=basis_code[g][:].bitcast(FP8X4),
-                scales=basis_scale[g][:],
-                in_=basis_grouped[g][:].rearrange("p t m j -> p (t m j)"),
+                out=basis_code[g, pair][:].bitcast(FP8X4),
+                scales=basis_scale[g, pair][:],
+                in_=basis_grouped[g, pair][:].rearrange("p t m j -> p (t m j)"),
             )
 
         log_brdf, brdf, f_grouped, f_code, f_scale = {}, {}, {}, {}, {}
@@ -189,8 +187,8 @@ def tile_log_brdf_environment_transport_k6_kernel(
         def stage1_pass(g, h, t, c):
             if c == 0:
                 log_brdf[g, h, t] = bank([P, 512])
-                weights = basis_code[g][:, P * t : P * (t + 1)].bitcast(FP8X4)
-                scales = basis_scale[g][:, P * t : P * (t + 1)]
+                weights = basis_code[g, t // 2][:, P * (t % 2) : P * (t % 2 + 1)].bitcast(FP8X4)
+                scales = basis_scale[g, t // 2][:, P * (t % 2) : P * (t % 2 + 1)]
             else:
                 weights = fine_code[g][:, t, c - 1, :].bitcast(FP4X4)
                 scales = fine_scale[g][:, t, c - 1, :]
@@ -205,32 +203,40 @@ def tile_log_brdf_environment_transport_k6_kernel(
                 brdf[g, h] = work.tile([P, 4, 512], F32, name="brdf", bufs=3)
             nc.scalar.activation(out=brdf[g, h][:, t, :], in_=log_brdf[g, h, t][:], func=ACT.Exp)
 
-        def weigh(g, h):
-            f_grouped[g, h] = work.tile([P, 2048], BF16, name="f_grouped", bufs=2, align_bytes=64)
+        def weigh(g, q):
+            h = q // 2
+            f_grouped[g, q] = work.tile([P, 1024], BF16, name="f_grouped", bufs=4, align_bytes=64)
             nc.vector.tensor_tensor(
-                out=f_grouped[g, h][:].rearrange("p (a r t) -> p a t r", r=4, t=4),
-                in0=brdf[g, h][:].rearrange("p t (a r) -> p a t r", r=4),
-                in1=cos_sb[:, g, :].rearrange("p (a t r) -> p a t r", a=1, r=1).to_broadcast([P, 128, 4, 4]),
+                out=f_grouped[g, q][:].rearrange("p (a r t) -> p a t r", r=4, t=4),
+                in0=brdf[g, h][:, :, 256 * (q % 2) : 256 * (q % 2 + 1)].rearrange("p t (a r) -> p a t r", r=4),
+                in1=cos_sb[:, g, :].rearrange("p (a t r) -> p a t r", a=1, r=1).to_broadcast([P, 64, 4, 4]),
                 op=ALU.mult,
             )
 
-        def quantize_f(g, h):
-            f_code[g, h] = kept("f_code_%d_%d" % (g, h), [P, 512], U32)
-            f_scale[g, h] = kept("f_scale_%d_%d" % (g, h), [P, 512], U8)
+        def quantize_f(g, q):
+            f_code[g, q] = kept("f_code_%d_%d" % (g, q), [P, 256], U32)
+            f_scale[g, q] = kept("f_scale_%d_%d" % (g, q), [P, 256], U8)
             nc.vector.quantize_mx(
-                out=f_code[g, h][:].bitcast(FP8X4), scales=f_scale[g, h][:], in_=f_grouped[g, h][:]
+                out=f_code[g, q][:].bitcast(FP8X4), scales=f_scale[g, q][:], in_=f_grouped[g, q][:]
             )
 
-        lit, y_sorted, y_grouped, y_code, accs = {}, {}, {}, {}, {}
+        def make_f(g, h):
+            for q in (2 * h, 2 * h + 1):
+                weigh(g, q)
+            for q in (2 * h, 2 * h + 1):
+                quantize_f(g, q)
+
+        y_rows = {}
+        lit, y_sorted, y_grouped, accs = {}, {}, {}, {}
 
         def stage2_pass(k, half, g):
-            h = k // 4
-            cols = slice(P * (k % 4), P * (k % 4 + 1))
+            q = k // 2
+            cols = slice(P * (k % 2), P * (k % 2 + 1))
             n = slice(512 * half, 512 * (half + 1))
             if g == 0:
                 accs[k, half] = bank([P, 512])
             nc.tensor.matmul_mx(
-                out=accs[k, half][:], lhsT=f_code[g, h][:, cols].bitcast(FP8X4), lhsT_scale=f_scale[g, h][:, cols],
+                out=accs[k, half][:], lhsT=f_code[g, q][:, cols].bitcast(FP8X4), lhsT_scale=f_scale[g, q][:, cols],
                 rhs=light[g][:, n].bitcast(FP8X4), rhs_scale=light_scale[:, g, n],
                 start=(g == 0), stop=(g == 2),
             )
@@ -238,7 +244,7 @@ def tile_log_brdf_environment_transport_k6_kernel(
         def tint_rows(k, half):
             q, i = divmod(k, 2)
             n = slice(512 * half, 512 * (half + 1))
-            lit[k, half] = work.tile([P, 512], F32, name="lit", bufs=4)
+            lit[k, half] = work.tile([P, 512], F32, name="lit", bufs=6)
             nc.vector.scalar_tensor_tensor(
                 out=lit[k, half][:], in0=accs[k, half][:], scalar=tint_sb[:, q, i : i + 1],
                 in1=bounce_sb[q][:, i, n], op0=ALU.mult, op1=ALU.add,
@@ -249,167 +255,179 @@ def tile_log_brdf_environment_transport_k6_kernel(
                 for g in range(3):
                     stage2_pass(k, half, g)
 
-        def finish_rows(k, half):
+        def finish_rows(k, half, engine=nc.gpsimd):
             q, i = divmod(k, 2)
             n = slice(512 * half, 512 * (half + 1))
             y = work.tile([P, 512], F32, name="y", bufs=6)
-            nc.vector.tensor_tensor(out=y[:], in0=lit[k, half][:], in1=power_sb[:, n], op=ALU.mult)
+            engine.tensor_tensor(out=y[:], in0=lit[k, half][:], in1=power_sb[:, n], op=ALU.mult)
             nc.sync.dma_start(
                 out=out_0[256 * q : 256 * (q + 1), n].rearrange("(p i) n -> p i n", i=2)[:, i, :], in_=y[:]
             )
+            y_rows[k, half] = y
+
+        def sort_rows(k, half):
+            y = y_rows[k, half]
             y_sorted[k, half] = work.tile([P, 512], BF16, name="y_sorted", bufs=8)
             nc.scalar.copy(
                 out=y_sorted[k, half][:].rearrange("p (u j e) -> p u j e", u=2, e=2),
                 in_=y[:].rearrange("p (j u e) -> p u j e", u=2, e=2),
             )
 
-        def epilogue(k):
+        def epilogue(k, engine):
             tint_rows(k, 0)
             tint_rows(k, 1)
-            finish_rows(k, 0)
-            finish_rows(k, 1)
+            finish_rows(k, 0, engine)
+            finish_rows(k, 1, engine)
 
-        def turn_y(q, g):
+        def sort_both(k):
+            sort_rows(k, 0)
+            sort_rows(k, 1)
+
+        def turn_y(q, g, copy=nc.scalar.copy):
             turned = bank([P, 2, 2, P])
             for i in range(2):
                 words = y_sorted[2 * q + i, g][:].bitcast(F32)
                 for u in range(2):
                     nc.tensor.transpose(turned[:, i, u, :], words[:, P * u : P * (u + 1)], ident[:])
             y_grouped[q, g] = work.tile([P, 1024], BF16, name="y_grouped", bufs=4, align_bytes=64)
-            nc.scalar.copy(
+            copy(
                 out=y_grouped[q, g][:].bitcast(F32).rearrange("p (r i u) -> p r i u", i=2, u=2),
                 in_=turned[:].rearrange("p i u r -> p r i u"),
             )
 
         def quantize_y(q, g):
             m = slice(256 * q, 256 * (q + 1))
-            y_code[q, g] = kept("y_code_%d_%d" % (q, g), [P, 256], U32)
-            nc.vector.quantize_mx(
-                out=y_code[q, g][:].bitcast(FP8X4), scales=y_scale[:, g, m], in_=y_grouped[q, g][:]
-            )
+            y_code = kept("y_code_%d_%d" % (q, g), [P, 256], U32)
+            nc.vector.quantize_mx(out=y_code[:].bitcast(FP8X4), scales=y_scale[:, g, m], in_=y_grouped[q, g][:])
             nc.sync.dma_start(
-                out=out_1[g, :, m, :].rearrange("p m t -> p (m t)").bitcast(I32), in_=y_code[q, g][:].bitcast(I32)
+                out=out_1[g, :, m, :].rearrange("p m t -> p (m t)").bitcast(I32), in_=y_code[:].bitcast(I32)
             )
 
-        def unit(g, h, beside=None):
-            for t in range(4):
+        def unit(g, h, slots=range(4)):
+            for t in slots:
                 for c in range(3):
                     stage1_pass(g, h, t, c)
                 exponentiate(g, h, t)
-                if beside is not None:
-                    beside(t)
+
+        def turn_pair(first, second):
+            turn_coef(*first)
+            turn_coef(*second)
 
         turn_coef(0, 0)
         turn_coef(0, 1)
         order_fine_scales(0)
         order_fine_codes(0)
+        group_basis(0, 0, nc.scalar.copy)
+        group_basis(0, 1, nc.scalar.copy)
         quantize_coef(0, 0)
         quantize_coef(0, 1)
-        group_basis(0, nc.vector.tensor_copy, 0, 1)
         order_fine_scales(1)
-        quantize_basis(0)
+        quantize_basis(0, 0)
+        order_fine_scales(2)
+        quantize_basis(0, 1)
         for q in range(2):
             for c in (1, 2):
                 turn_coef(c, q)
         for q in range(2):
             for c in (1, 2):
                 quantize_coef(c, q)
+        group_basis(1, 1, nc.scalar.copy)
+        group_basis(1, 0, nc.vector.tensor_copy)
+        order_fine_codes(1)
+        quantize_basis(1, 0)
+        quantize_basis(1, 1)
+        group_basis(2, 1, nc.scalar.copy)
+        group_basis(2, 0, nc.vector.tensor_copy)
+        order_fine_codes(2)
+        quantize_basis(2, 0)
+        quantize_basis(2, 1)
         for t in range(4):
             stage1_pass(0, 0, t, 0)
-        group_basis(1, nc.scalar.copy, 0, 1)
-        order_fine_codes(1)
-        order_fine_scales(2)
-        quantize_basis(1)
-        order_fine_codes(2)
         for t in range(4):
             for c in (1, 2):
                 stage1_pass(0, 0, t, c)
             exponentiate(0, 0, t)
-        turn_coef(0, 2)
-        turn_coef(0, 3)
-        group_basis(2, nc.vector.tensor_copy, 0, 1)
+        turn_pair((0, 2), (0, 3))
+        unit(1, 0, (0, 1))
+        turn_pair((1, 2), (2, 2))
+        unit(1, 0, (2, 3))
+        turn_pair((1, 3), (2, 3))
         weigh(0, 0)
-        quantize_basis(2)
-        quantize_coef(0, 2)
-        quantize_coef(0, 3)
-        quantize_f(0, 0)
-        unit(1, 0)
-        for q in (2, 3):
-            for c in (1, 2):
-                turn_coef(c, q)
-        weigh(1, 0)
-        for q in (2, 3):
-            for c in (1, 2):
-                quantize_coef(c, q)
-        quantize_f(1, 0)
-        unit(2, 0)
-        weigh(2, 0)
-        unit(0, 1)
-        quantize_f(2, 0)
-        stage2(0)
         weigh(0, 1)
-        unit(1, 1)
-        tint_rows(0, 0)
+        quantize_coef(0, 2)
+        quantize_f(0, 0)
         quantize_f(0, 1)
-        tint_rows(0, 1)
-        stage2(1)
-        finish_rows(0, 0)
-        finish_rows(0, 1)
+        quantize_coef(0, 3)
+        quantize_coef(1, 2)
+        quantize_coef(2, 2)
+        weigh(1, 0)
+        quantize_coef(1, 3)
+        quantize_coef(2, 3)
         weigh(1, 1)
-        stage2(2)
-        tint_rows(1, 0)
+        unit(2, 0)
+        quantize_f(1, 0)
         quantize_f(1, 1)
-        tint_rows(1, 1)
+        unit(0, 1)
+        make_f(2, 0)
+        stage2(0)
+        stage2(1)
+        make_f(0, 1)
+        epilogue(0, nc.vector)
+        epilogue(1, nc.vector)
+        unit(1, 1)
+        sort_both(0)
+        sort_both(1)
+        stage2(2)
+        make_f(1, 1)
+        epilogue(2, nc.vector)
         unit(2, 1)
-        finish_rows(1, 0)
-        finish_rows(1, 1)
-        tint_rows(2, 0)
-        tint_rows(2, 1)
-        stage2(3)
         turn_y(0, 0)
         turn_y(0, 1)
-        weigh(2, 1)
-        finish_rows(2, 0)
-        quantize_f(2, 1)
-        finish_rows(2, 1)
+        sort_both(2)
+        stage2(3)
         for k in (4, 5):
             for half in range(2):
-                for g in range(3):
+                for g in range(2):
                     stage2_pass(k, half, g)
-        tint_rows(3, 0)
-        tint_rows(3, 1)
+        make_f(2, 1)
         quantize_y(0, 0)
         quantize_y(0, 1)
-        finish_rows(3, 0)
-        finish_rows(3, 1)
-        epilogue(4)
+        for k in (4, 5):
+            for half in range(2):
+                stage2_pass(k, half, 2)
+        epilogue(3, nc.gpsimd)
+        sort_both(3)
+        epilogue(4, nc.gpsimd)
+        tint_rows(5, 0)
+        tint_rows(5, 1)
+        finish_rows(5, 0)
+        for half in range(2):
+            for k in (6, 7):
+                for g in range(3):
+                    stage2_pass(k, half, g)
         turn_y(1, 0)
         turn_y(1, 1)
-        for k in (6, 7):
-            for g in range(3):
-                stage2_pass(k, 0, g)
-        epilogue(5)
-        quantize_y(1, 0)
-        quantize_y(1, 1)
-        for k in (6, 7):
-            for g in range(3):
-                stage2_pass(k, 1, g)
-        turn_y(2, 0)
-        turn_y(2, 1)
+        sort_both(4)
         for half in range(2):
             tint_rows(6, half)
             tint_rows(7, half)
-            finish_rows(6, half)
-            finish_rows(7, half)
-            if half == 0:
-                turn_y(3, 0)
-        quantize_y(2, 0)
-        quantize_y(2, 1)
-        quantize_y(3, 0)
+        last = ((5, 1), (6, 0), (7, 0), (6, 1), (7, 1))
+        for k, half in last:
+            finish_rows(k, half, nc.vector)
+        sort_rows(5, 0)
+        for k, half in last:
+            sort_rows(k, half)
+        quantize_y(1, 0)
+        quantize_y(1, 1)
+        turn_y(2, 0, nc.vector.tensor_copy)
+        turn_y(2, 1, nc.vector.tensor_copy)
+        turn_y(3, 0)
         turn_y(3, 1)
-        quantize_y(3, 1)
+        for q in (2, 3):
+            quantize_y(q, 0)
+            quantize_y(q, 1)
         for quad in range(4):
-            nc.sync.dma_start(
+            nc.scalar.dma_start(
                 out=out_2[:, 4 * quad : 4 * quad + 4, :].rearrange("g r m -> r g m").bitcast(I32),
                 in_=y_scale[32 * quad : 32 * quad + 4, :, :].bitcast(I32),
             )

@@ -83,21 +83,21 @@ def tile_log_brdf_environment_transport_k6_kernel(
             )
 
         load_lead(0)
+        load_words(0)
+        load_basis(0)
+        load_fine(0)
+        load_fine(1)
         for quad in range(4):
             nc.sync.dma_start(
                 out=fine_scale_raw[32 * quad : 32 * quad + 4, :, :].bitcast(I32),
                 in_=fine_scales[:, 4 * quad : 4 * quad + 4, :].rearrange("k r n -> r k n").bitcast(I32),
             )
-        load_words(0)
-        load_basis(0)
-        load_fine(0)
-        load_fine(1)
         load_words(1)
         load_basis(1)
         load_words(2)
+        load_lead(1)
         load_basis(2)
         nc.sync.dma_start(out=cos_sb[:], in_=cos_weight.rearrange("(g p t) -> p g t", g=3, t=4))
-        load_lead(1)
         load_fine(2)
         load_fine(3)
         for quad in range(4):
@@ -167,7 +167,7 @@ def tile_log_brdf_environment_transport_k6_kernel(
             )
 
         def group_basis(g, pair, copy):
-            basis_grouped[g, pair] = kept("basis_grouped_%d_%d" % (g, pair), [P, 2, P, 4], BF16)
+            basis_grouped[g, pair] = work.tile([P, 2, P, 4], BF16, name="basis_grouped", bufs=3, align_bytes=64)
             copy(
                 out=basis_grouped[g, pair][:].rearrange("p t (a m) j -> p a t m j", m=2),
                 in_=basis_raw[g][:].rearrange("p j (a m t) -> p a t m j", m=2, t=4)[:, :, 2 * pair : 2 * pair + 2],
@@ -213,6 +213,23 @@ def tile_log_brdf_environment_transport_k6_kernel(
                 op=ALU.mult,
             )
 
+        f_rows = {}
+        cos_f32 = kept("cos_f32", [P, 3, 4], F32)
+
+        def scale_rows(g, h, t):
+            if t == 0:
+                f_rows[g, h] = work.tile([P, 4, 512], BF16, name="f_rows", bufs=1)
+            nc.scalar.activation(
+                out=f_rows[g, h][:, t, :], in_=brdf[g, h][:, t, :], func=ACT.Copy, scale=cos_f32[:, g, t : t + 1]
+            )
+
+        def group_f(g, q):
+            f_grouped[g, q] = work.tile([P, 1024], BF16, name="f_grouped", bufs=4, align_bytes=64)
+            nc.vector.tensor_copy(
+                out=f_grouped[g, q][:].rearrange("p (a r t) -> p a t r", r=4, t=4),
+                in_=f_rows[g, q // 2][:, :, 256 * (q % 2) : 256 * (q % 2 + 1)].rearrange("p t (a r) -> p a t r", r=4),
+            )
+
         def quantize_f(g, q):
             f_code[g, q] = kept("f_code_%d_%d" % (g, q), [P, 256], U32)
             f_scale[g, q] = kept("f_scale_%d_%d" % (g, q), [P, 256], U8)
@@ -244,7 +261,7 @@ def tile_log_brdf_environment_transport_k6_kernel(
         def tint_rows(k, half):
             q, i = divmod(k, 2)
             n = slice(512 * half, 512 * (half + 1))
-            lit[k, half] = work.tile([P, 512], F32, name="lit", bufs=6)
+            lit[k, half] = work.tile([P, 512], F32, name="lit", bufs=8)
             nc.vector.scalar_tensor_tensor(
                 out=lit[k, half][:], in0=accs[k, half][:], scalar=tint_sb[:, q, i : i + 1],
                 in1=bounce_sb[q][:, i, n], op0=ALU.mult, op1=ALU.add,
@@ -303,6 +320,14 @@ def tile_log_brdf_environment_transport_k6_kernel(
                 out=out_1[g, :, m, :].rearrange("p m t -> p (m t)").bitcast(I32), in_=y_code[:].bitcast(I32)
             )
 
+        def store_scales(h, queue):
+            m = slice(512 * h, 512 * (h + 1))
+            for quad in range(4):
+                queue.dma_start(
+                    out=out_2[:, 4 * quad : 4 * quad + 4, m].rearrange("g r m -> r g m").bitcast(I32),
+                    in_=y_scale[32 * quad : 32 * quad + 4, :, m].bitcast(I32),
+                )
+
         def unit(g, h, slots=range(4)):
             for t in slots:
                 for c in range(3):
@@ -313,69 +338,82 @@ def tile_log_brdf_environment_transport_k6_kernel(
             turn_coef(*first)
             turn_coef(*second)
 
-        turn_coef(0, 0)
-        turn_coef(0, 1)
-        order_fine_scales(0)
+        def helped_unit(g, h):
+            for t in range(4):
+                unit(g, h, (t,))
+                if t:
+                    scale_rows(g, h, t - 1)
+            scale_rows(g, h, 3)
+
+        turn_pair((0, 0), (0, 1))
         order_fine_codes(0)
-        group_basis(0, 0, nc.scalar.copy)
         group_basis(0, 1, nc.scalar.copy)
         quantize_coef(0, 0)
         quantize_coef(0, 1)
-        order_fine_scales(1)
-        quantize_basis(0, 0)
-        order_fine_scales(2)
+        group_basis(0, 0, nc.vector.tensor_copy)
+        turn_pair((1, 0), (2, 0))
+        turn_pair((1, 1), (2, 1))
         quantize_basis(0, 1)
-        for q in range(2):
-            for c in (1, 2):
-                turn_coef(c, q)
-        for q in range(2):
-            for c in (1, 2):
-                quantize_coef(c, q)
+        quantize_basis(0, 0)
+        quantize_coef(1, 0)
+        quantize_coef(2, 0)
+        order_fine_scales(0)
+        quantize_coef(1, 1)
+        quantize_coef(2, 1)
+        group_basis(1, 0, nc.scalar.copy)
         group_basis(1, 1, nc.scalar.copy)
-        group_basis(1, 0, nc.vector.tensor_copy)
         order_fine_codes(1)
+        order_fine_scales(1)
+        order_fine_codes(2)
         quantize_basis(1, 0)
         quantize_basis(1, 1)
-        group_basis(2, 1, nc.scalar.copy)
-        group_basis(2, 0, nc.vector.tensor_copy)
-        order_fine_codes(2)
-        quantize_basis(2, 0)
-        quantize_basis(2, 1)
         for t in range(4):
             stage1_pass(0, 0, t, 0)
         for t in range(4):
             for c in (1, 2):
                 stage1_pass(0, 0, t, c)
             exponentiate(0, 0, t)
+        order_fine_scales(2)
+        group_basis(2, 0, nc.vector.tensor_copy)
         turn_pair((0, 2), (0, 3))
         unit(1, 0, (0, 1))
+        group_basis(2, 1, nc.scalar.copy)
         turn_pair((1, 2), (2, 2))
         unit(1, 0, (2, 3))
         turn_pair((1, 3), (2, 3))
         weigh(0, 0)
+        quantize_basis(2, 0)
         weigh(0, 1)
-        quantize_coef(0, 2)
         quantize_f(0, 0)
+        quantize_basis(2, 1)
         quantize_f(0, 1)
+        quantize_coef(0, 2)
         quantize_coef(0, 3)
         quantize_coef(1, 2)
         quantize_coef(2, 2)
         weigh(1, 0)
+        weigh(1, 1)
         quantize_coef(1, 3)
         quantize_coef(2, 3)
-        weigh(1, 1)
         unit(2, 0)
         quantize_f(1, 0)
         quantize_f(1, 1)
-        unit(0, 1)
+        nc.scalar.copy(out=cos_f32[:], in_=cos_sb[:])
+        helped_unit(0, 1)
         make_f(2, 0)
         stage2(0)
         stage2(1)
-        make_f(0, 1)
         epilogue(0, nc.vector)
-        epilogue(1, nc.vector)
-        unit(1, 1)
+        group_f(0, 2)
+        group_f(0, 3)
+        tint_rows(1, 0)
+        quantize_f(0, 2)
+        quantize_f(0, 3)
+        tint_rows(1, 1)
+        finish_rows(1, 0, nc.vector)
+        finish_rows(1, 1, nc.vector)
         sort_both(0)
+        unit(1, 1)
         sort_both(1)
         stage2(2)
         make_f(1, 1)
@@ -400,25 +438,23 @@ def tile_log_brdf_environment_transport_k6_kernel(
         epilogue(4, nc.gpsimd)
         tint_rows(5, 0)
         tint_rows(5, 1)
-        finish_rows(5, 0)
         for half in range(2):
             for k in (6, 7):
                 for g in range(3):
                     stage2_pass(k, half, g)
-        turn_y(1, 0)
-        turn_y(1, 1)
-        sort_both(4)
+            turn_y(1, half)
+            sort_rows(4, half)
         for half in range(2):
             tint_rows(6, half)
             tint_rows(7, half)
-        last = ((5, 1), (6, 0), (7, 0), (6, 1), (7, 1))
+        last = ((5, 0), (5, 1), (6, 0), (7, 0), (6, 1), (7, 1))
         for k, half in last:
             finish_rows(k, half, nc.vector)
-        sort_rows(5, 0)
         for k, half in last:
             sort_rows(k, half)
         quantize_y(1, 0)
         quantize_y(1, 1)
+        store_scales(0, nc.sync)
         turn_y(2, 0, nc.vector.tensor_copy)
         turn_y(2, 1, nc.vector.tensor_copy)
         turn_y(3, 0)
@@ -426,8 +462,4 @@ def tile_log_brdf_environment_transport_k6_kernel(
         for q in (2, 3):
             quantize_y(q, 0)
             quantize_y(q, 1)
-        for quad in range(4):
-            nc.scalar.dma_start(
-                out=out_2[:, 4 * quad : 4 * quad + 4, :].rearrange("g r m -> r g m").bitcast(I32),
-                in_=y_scale[32 * quad : 32 * quad + 4, :, :].bitcast(I32),
-            )
+        store_scales(1, nc.scalar)

@@ -312,21 +312,16 @@ def tile_log_brdf_environment_transport_k6_kernel(
                 in_=turned[:].rearrange("p i u r -> p r i u"),
             )
 
-        def quantize_y(q, g):
+        def quantize_y(q):
             m = slice(256 * q, 256 * (q + 1))
-            y_code = kept("y_code_%d_%d" % (q, g), [P, 256], U32)
-            nc.vector.quantize_mx(out=y_code[:].bitcast(FP8X4), scales=y_scale[:, g, m], in_=y_grouped[q, g][:])
-            nc.sync.dma_start(
-                out=out_1[g, :, m, :].rearrange("p m t -> p (m t)").bitcast(I32), in_=y_code[:].bitcast(I32)
-            )
-
-        def store_scales(h, queue):
-            m = slice(512 * h, 512 * (h + 1))
-            for quad in range(4):
-                queue.dma_start(
-                    out=out_2[:, 4 * quad : 4 * quad + 4, m].rearrange("g r m -> r g m").bitcast(I32),
-                    in_=y_scale[32 * quad : 32 * quad + 4, :, m].bitcast(I32),
+            y_code = kept("y_code_%d" % q, [P, 2, 256], U32)
+            for g in range(2):
+                nc.vector.quantize_mx(
+                    out=y_code[:, g, :].bitcast(FP8X4), scales=y_scale[:, g, m], in_=y_grouped[q, g][:]
                 )
+            nc.sync.dma_start(
+                out=out_1[:, :, m, :].rearrange("g p m t -> p g (m t)").bitcast(I32), in_=y_code[:].bitcast(I32)
+            )
 
         def unit(g, h, slots=range(4)):
             for t in slots:
@@ -428,8 +423,7 @@ def tile_log_brdf_environment_transport_k6_kernel(
                 for g in range(2):
                     stage2_pass(k, half, g)
         make_f(2, 1)
-        quantize_y(0, 0)
-        quantize_y(0, 1)
+        quantize_y(0)
         for k in (4, 5):
             for half in range(2):
                 stage2_pass(k, half, 2)
@@ -452,14 +446,15 @@ def tile_log_brdf_environment_transport_k6_kernel(
             finish_rows(k, half, nc.vector)
         for k, half in last:
             sort_rows(k, half)
-        quantize_y(1, 0)
-        quantize_y(1, 1)
-        store_scales(0, nc.sync)
+        quantize_y(1)
         turn_y(2, 0, nc.vector.tensor_copy)
         turn_y(2, 1, nc.vector.tensor_copy)
         turn_y(3, 0)
         turn_y(3, 1)
-        for q in (2, 3):
-            quantize_y(q, 0)
-            quantize_y(q, 1)
-        store_scales(1, nc.scalar)
+        quantize_y(2)
+        quantize_y(3)
+        for quad in range(4):
+            nc.scalar.dma_start(
+                out=out_2[:, 4 * quad : 4 * quad + 4, :].rearrange("g r m -> r g m").bitcast(I32),
+                in_=y_scale[32 * quad : 32 * quad + 4, :, :].bitcast(I32),
+            )

@@ -3,8 +3,8 @@ from contextlib import ExitStack
 import concourse.mybir as mybir
 from concourse.masks import make_identity
 
-R, K1, K2, D, NL = 1024, 512, 1024, 1536, 1024
-FLOPS = 2 * R * (K1 + K2) * D + 2 * R * D * NL
+TEXELS, LEAD, FINE, BINS, PATTERNS = 1024, 512, 1024, 1536, 1024
+FLOPS = 2 * TEXELS * (LEAD + FINE) * BINS + 2 * TEXELS * BINS * PATTERNS
 
 F32 = mybir.dt.float32
 BF16 = mybir.dt.bfloat16
@@ -17,7 +17,8 @@ ACT = mybir.ActivationFunctionType
 ALU = mybir.AluOpType
 
 P = 128
-KP = 512
+SPAN = 512
+QUARTER = 256
 
 
 def tile_log_brdf_environment_transport_k6_kernel(
@@ -39,86 +40,89 @@ def tile_log_brdf_environment_transport_k6_kernel(
 
         ident = kept("ident", [P, P], F32)
         warm = kept("warm", [P, 16], F32)
-        fine_scale_raw = kept("fine_scale_raw", [P, 2, D], U8)
-        light_scale = kept("light_scale", [P, 3, NL], U8)
+        first_scale_raw = kept("first_scale_raw", [P, 2, SPAN], U8)
+        later_scale_raw = kept("later_scale_raw", [P, 2, BINS - SPAN], U8)
+        light_scale = kept("light_scale", [P, 3, PATTERNS], U8)
         cos_sb = kept("cos_sb", [P, 3, 4], BF16)
         tint_sb = kept("tint_sb", [P, 4, 2], BF16)
-        power_sb = kept("power_sb", [P, NL], BF16)
-        y_scale = kept("y_scale", [P, 2, R], U8)
+        power_sb = kept("power_sb", [P, PATTERNS], BF16)
+        y_scale = kept("y_scale", [P, TEXELS], U8)
 
         make_identity(nc, ident[:])
-        nc.vector.memset(fine_scale_raw[:].bitcast(I32), 0)
+        nc.vector.memset(first_scale_raw[:].bitcast(I32), 0)
         nc.vector.memset(warm[:], 0.0)
+        nc.vector.memset(later_scale_raw[:].bitcast(I32), 0)
         nc.vector.memset(light_scale[:].bitcast(I32), 0)
         nc.scalar.activation(out=warm[:, 8:9], in_=warm[:, 0:1], func=ACT.Exp)
 
-        lead_raw, fine_coef_raw, basis_raw, fine_raw, light, bounce_sb = {}, {}, {}, {}, {}, {}
+        lead_raw, fine_coef_raw, basis_raw, fine_word_raw, light, bounce_sb = {}, {}, {}, {}, {}, {}
 
         def load_lead(h):
-            lead_raw[h] = kept("lead_raw_%d" % h, [P, 2, 2 * K1], BF16)
+            lead_raw[h] = kept("lead_raw_%d" % h, [P, 2, 2 * LEAD], BF16)
             nc.sync.dma_start(
                 out=lead_raw[h][:],
-                in_=coef_lead[512 * h : 512 * (h + 1), :].rearrange("(q p i) k -> p q (i k)", q=2, i=2),
+                in_=coef_lead[SPAN * h : SPAN * (h + 1), :].rearrange("(q p i) k -> p q (i k)", q=2, i=2),
             )
 
-        def load_fine(q):
-            fine_coef_raw[q] = kept("fine_coef_raw_%d" % q, [P, 2 * K2], BF16)
+        def load_fine_coef(q):
+            fine_coef_raw[q] = kept("fine_coef_raw_%d" % q, [P, 2 * FINE], BF16)
             nc.sync.dma_start(
                 out=fine_coef_raw[q][:],
-                in_=coef_fine[256 * q : 256 * (q + 1), :].rearrange("(p i) k -> p (i k)", i=2),
+                in_=coef_fine[QUARTER * q : QUARTER * (q + 1), :].rearrange("(p i) k -> p (i k)", i=2),
             )
 
-        def load_words(g):
-            fine_raw[g] = kept("fine_raw_%d" % g, [P, 2, 2 * KP], U8)
+        def load_fine_words(g):
+            fine_word_raw[g] = kept("fine_word_raw_%d" % g, [P, 2, 2 * SPAN], U8)
             nc.sync.dma_start(
-                out=fine_raw[g][:].bitcast(I32),
-                in_=fine_words[:, :, 2 * KP * g : 2 * KP * (g + 1)].rearrange("k p b -> p k b").bitcast(I32),
+                out=fine_word_raw[g][:].bitcast(I32),
+                in_=fine_words[:, :, 2 * SPAN * g : 2 * SPAN * (g + 1)].rearrange("c p b -> p c b").bitcast(I32),
             )
 
         def load_basis(g):
-            basis_raw[g] = kept("basis_raw_%d" % g, [P, 4, KP], BF16)
+            basis_raw[g] = kept("basis_raw_%d" % g, [P, 4, SPAN], BF16)
             nc.sync.dma_start(
                 out=basis_raw[g][:],
-                in_=basis_lead[:, KP * g : KP * (g + 1)].rearrange("(p j) d -> p j d", j=4),
+                in_=basis_lead[:, SPAN * g : SPAN * (g + 1)].rearrange("(p j) d -> p j d", j=4),
             )
 
+        def load_scale_rows(plane, rows):
+            for n in range(4):
+                nc.sync.dma_start(
+                    out=plane[32 * n : 32 * n + 4, :, :].bitcast(I32),
+                    in_=rows[:, 4 * n : 4 * n + 4, :].rearrange("c r d -> r c d").bitcast(I32),
+                )
+
         load_lead(0)
-        load_words(0)
+        load_scale_rows(first_scale_raw, fine_scales[:, :, 0:SPAN])
+        load_fine_words(0)
         load_basis(0)
-        load_fine(0)
-        load_fine(1)
-        for quad in range(4):
-            nc.sync.dma_start(
-                out=fine_scale_raw[32 * quad : 32 * quad + 4, :, :].bitcast(I32),
-                in_=fine_scales[:, 4 * quad : 4 * quad + 4, :].rearrange("k r n -> r k n").bitcast(I32),
-            )
-        load_words(1)
+        load_fine_coef(0)
+        load_fine_coef(1)
+        load_fine_words(1)
         load_basis(1)
-        load_words(2)
+        load_scale_rows(later_scale_raw, fine_scales[:, :, SPAN:BINS])
+        load_fine_words(2)
         load_lead(1)
         load_basis(2)
         nc.sync.dma_start(out=cos_sb[:], in_=cos_weight.rearrange("(g p t) -> p g t", g=3, t=4))
-        load_fine(2)
-        load_fine(3)
-        for quad in range(4):
-            nc.sync.dma_start(
-                out=light_scale[32 * quad : 32 * quad + 4, :, :].bitcast(I32),
-                in_=light_scales[:, 4 * quad : 4 * quad + 4, :].rearrange("g r n -> r g n").bitcast(I32),
-            )
+        load_fine_coef(2)
+        load_fine_coef(3)
+        load_scale_rows(light_scale, light_scales)
         for g in range(3):
-            light[g] = kept("light_%d" % g, [P, NL], U32)
+            light[g] = kept("light_%d" % g, [P, PATTERNS], U32)
             nc.sync.dma_start(
                 out=light[g][:].bitcast(I32),
                 in_=light_words[g].rearrange("p n t -> p (n t)").bitcast(I32),
             )
         nc.sync.dma_start(out=tint_sb[:], in_=tint.rearrange("(q p i) -> p q i", q=4, i=2))
-        nc.sync.dma_start(out=power_sb[:], in_=power.partition_broadcast(P))
         for q in range(4):
-            bounce_sb[q] = kept("bounce_%d" % q, [P, 2, NL], BF16)
+            bounce_sb[q] = kept("bounce_%d" % q, [P, 2, PATTERNS], BF16)
             nc.sync.dma_start(
                 out=bounce_sb[q][:],
-                in_=bounce[256 * q : 256 * (q + 1), :].rearrange("(p i) n -> p i n", i=2),
+                in_=bounce[QUARTER * q : QUARTER * (q + 1), :].rearrange("(p i) n -> p i n", i=2),
             )
+            if q == 0:
+                nc.sync.dma_start(out=power_sb[:], in_=power.partition_broadcast(P))
 
         coef_grouped, coef_code, coef_scale = {}, {}, {}
 
@@ -126,24 +130,28 @@ def tile_log_brdf_environment_transport_k6_kernel(
             turned = bank([P, 2, 2, P])
             for i in range(2):
                 if c == 0:
-                    words = lead_raw[q // 2][:, q % 2, :].bitcast(F32)[:, 256 * i : 256 * (i + 1)]
+                    words = lead_raw[q // 2][:, q % 2, :].bitcast(F32)[:, QUARTER * i : QUARTER * (i + 1)]
                 else:
-                    first = 512 * i + 256 * (c - 1)
-                    words = fine_coef_raw[q][:].bitcast(F32)[:, first : first + 256]
+                    first = FINE // 2 * i + QUARTER * (c - 1)
+                    words = fine_coef_raw[q][:].bitcast(F32)[:, first : first + QUARTER]
                 for u in range(2):
-                    nc.tensor.transpose(turned[:, i, u, :], words[:, u:256:2], ident[:])
-            coef_grouped[c, q] = work.tile([P, 1024], BF16, name="coef_grouped", bufs=6, align_bytes=64)
+                    nc.tensor.transpose(turned[:, i, u, :], words[:, u:QUARTER:2], ident[:])
+            coef_grouped[c, q] = work.tile([P, 4 * QUARTER], BF16, name="coef_grouped", bufs=6, align_bytes=64)
             nc.scalar.copy(
                 out=coef_grouped[c, q][:].bitcast(F32).rearrange("p (i r u) -> p i r u", i=2, u=2),
                 in_=turned[:].rearrange("p i u r -> p i r u"),
             )
 
+        def turn_pair(first, second):
+            turn_coef(*first)
+            turn_coef(*second)
+
         def quantize_coef(c, q):
             h = q // 2
             if q % 2 == 0:
-                coef_code[c, h] = kept("coef_code_%d_%d" % (c, h), [P, 512], U32)
-                coef_scale[c, h] = kept("coef_scale_%d_%d" % (c, h), [P, 512], U8)
-            cols = slice(256 * (q % 2), 256 * (q % 2 + 1))
+                coef_code[c, h] = kept("coef_code_%d_%d" % (c, h), [P, SPAN], U32)
+                coef_scale[c, h] = kept("coef_scale_%d_%d" % (c, h), [P, SPAN], U8)
+            cols = slice(QUARTER * (q % 2), QUARTER * (q % 2 + 1))
             nc.vector.quantize_mx(
                 out=coef_code[c, h][:, cols].bitcast(FP8X4),
                 scales=coef_scale[c, h][:, cols],
@@ -155,15 +163,16 @@ def tile_log_brdf_environment_transport_k6_kernel(
         def order_fine_codes(g):
             fine_code[g] = kept("fine_code_%d" % g, [P, 4, 2, 2 * P], U8)
             nc.vector.tensor_copy(
-                out=fine_code[g][:].rearrange("p t k (a m b) -> p (k a) t m b", m=8, b=2),
-                in_=fine_raw[g][:].rearrange("p k (a m t b) -> p (k a) t m b", m=8, t=4, b=2),
+                out=fine_code[g][:].rearrange("p t c (a m b) -> p (c a) t m b", m=8, b=2),
+                in_=fine_word_raw[g][:].rearrange("p c (a m t b) -> p (c a) t m b", m=8, t=4, b=2),
             )
 
         def order_fine_scales(g):
+            raw = first_scale_raw[:] if g == 0 else later_scale_raw[:, :, SPAN * (g - 1) : SPAN * g]
             fine_scale[g] = kept("fine_scale_%d" % g, [P, 4, 2, P], U8)
             nc.vector.tensor_copy(
-                out=fine_scale[g][:].rearrange("p t k (a m) -> p k a t m", m=16),
-                in_=fine_scale_raw[:, :, KP * g : KP * (g + 1)].rearrange("p k (a m t) -> p k a t m", m=16, t=4),
+                out=fine_scale[g][:].rearrange("p t c (a m) -> p c a t m", m=16),
+                in_=raw.rearrange("p c (a m t) -> p c a t m", m=16, t=4),
             )
 
         def group_basis(g, pair, copy):
@@ -186,7 +195,7 @@ def tile_log_brdf_environment_transport_k6_kernel(
 
         def stage1_pass(g, h, t, c):
             if c == 0:
-                log_brdf[g, h, t] = bank([P, 512])
+                log_brdf[g, h, t] = bank([P, SPAN])
                 weights = basis_code[g, t // 2][:, P * (t % 2) : P * (t % 2 + 1)].bitcast(FP8X4)
                 scales = basis_scale[g, t // 2][:, P * (t % 2) : P * (t % 2 + 1)]
             else:
@@ -200,39 +209,51 @@ def tile_log_brdf_environment_transport_k6_kernel(
 
         def exponentiate(g, h, t):
             if t == 0:
-                brdf[g, h] = work.tile([P, 4, 512], F32, name="brdf", bufs=3)
+                brdf[g, h] = work.tile([P, 4, SPAN], F32, name="brdf", bufs=3)
             nc.scalar.activation(out=brdf[g, h][:, t, :], in_=log_brdf[g, h, t][:], func=ACT.Exp)
 
+        def unit(g, h, slots=range(4)):
+            for t in slots:
+                for c in range(3):
+                    stage1_pass(g, h, t, c)
+                exponentiate(g, h, t)
+
+        def quarter_cols(q):
+            return slice(QUARTER * (q % 2), QUARTER * (q % 2 + 1))
+
+        def new_f_grouped(g, q):
+            f_grouped[g, q] = work.tile([P, 4 * QUARTER], BF16, name="f_grouped", bufs=4, align_bytes=64)
+            return f_grouped[g, q][:].rearrange("p (a r t) -> p a t r", r=4, t=4)
+
         def weigh(g, q):
-            h = q // 2
-            f_grouped[g, q] = work.tile([P, 1024], BF16, name="f_grouped", bufs=4, align_bytes=64)
             nc.vector.tensor_tensor(
-                out=f_grouped[g, q][:].rearrange("p (a r t) -> p a t r", r=4, t=4),
-                in0=brdf[g, h][:, :, 256 * (q % 2) : 256 * (q % 2 + 1)].rearrange("p t (a r) -> p a t r", r=4),
-                in1=cos_sb[:, g, :].rearrange("p (a t r) -> p a t r", a=1, r=1).to_broadcast([P, 64, 4, 4]),
+                out=new_f_grouped(g, q),
+                in0=brdf[g, q // 2][:, :, quarter_cols(q)].rearrange("p t (a r) -> p a t r", r=4),
+                in1=cos_sb[:, g, :].rearrange("p (a t r) -> p a t r", a=1, r=1).to_broadcast([P, QUARTER // 4, 4, 4]),
                 op=ALU.mult,
             )
 
-        f_rows = {}
         cos_f32 = kept("cos_f32", [P, 3, 4], F32)
 
-        def scale_rows(g, h, t):
-            if t == 0:
-                f_rows[g, h] = work.tile([P, 4, 512], BF16, name="f_rows", bufs=1)
-            nc.scalar.activation(
-                out=f_rows[g, h][:, t, :], in_=brdf[g, h][:, t, :], func=ACT.Copy, scale=cos_f32[:, g, t : t + 1]
-            )
+        def unit_weighed_on_scalar(g, h):
+            unit(g, h, (0, 1))
+            rows = work.tile([P, 4, SPAN], BF16, name="f_rows", bufs=1)
+            for t in range(4):
+                nc.scalar.activation(
+                    out=rows[:, t, :], in_=brdf[g, h][:, t, :], func=ACT.Copy, scale=cos_f32[:, g, t : t + 1]
+                )
+                if t + 2 < 4:
+                    unit(g, h, (t + 2,))
+            return rows
 
-        def group_f(g, q):
-            f_grouped[g, q] = work.tile([P, 1024], BF16, name="f_grouped", bufs=4, align_bytes=64)
+        def group_f(g, q, rows):
             nc.vector.tensor_copy(
-                out=f_grouped[g, q][:].rearrange("p (a r t) -> p a t r", r=4, t=4),
-                in_=f_rows[g, q // 2][:, :, 256 * (q % 2) : 256 * (q % 2 + 1)].rearrange("p t (a r) -> p a t r", r=4),
+                out=new_f_grouped(g, q), in_=rows[:, :, quarter_cols(q)].rearrange("p t (a r) -> p a t r", r=4)
             )
 
         def quantize_f(g, q):
-            f_code[g, q] = kept("f_code_%d_%d" % (g, q), [P, 256], U32)
-            f_scale[g, q] = kept("f_scale_%d_%d" % (g, q), [P, 256], U8)
+            f_code[g, q] = kept("f_code_%d_%d" % (g, q), [P, QUARTER], U32)
+            f_scale[g, q] = kept("f_scale_%d_%d" % (g, q), [P, QUARTER], U8)
             nc.vector.quantize_mx(
                 out=f_code[g, q][:].bitcast(FP8X4), scales=f_scale[g, q][:], in_=f_grouped[g, q][:]
             )
@@ -243,102 +264,90 @@ def tile_log_brdf_environment_transport_k6_kernel(
             for q in (2 * h, 2 * h + 1):
                 quantize_f(g, q)
 
-        y_rows = {}
-        lit, y_sorted, y_grouped, accs = {}, {}, {}, {}
+        reflected, lit, y_rows, y_sorted, y_grouped, y_code = {}, {}, {}, {}, {}, {}
 
-        def stage2_pass(k, half, g):
-            q = k // 2
-            cols = slice(P * (k % 2), P * (k % 2 + 1))
-            n = slice(512 * half, 512 * (half + 1))
+        def side_cols(s):
+            return slice(SPAN * s, SPAN * (s + 1))
+
+        def stage2_pass(rt, s, g):
+            q, i = divmod(rt, 2)
+            texels = slice(P * i, P * (i + 1))
             if g == 0:
-                accs[k, half] = bank([P, 512])
+                reflected[rt, s] = bank([P, SPAN])
             nc.tensor.matmul_mx(
-                out=accs[k, half][:], lhsT=f_code[g, q][:, cols].bitcast(FP8X4), lhsT_scale=f_scale[g, q][:, cols],
-                rhs=light[g][:, n].bitcast(FP8X4), rhs_scale=light_scale[:, g, n],
+                out=reflected[rt, s][:],
+                lhsT=f_code[g, q][:, texels].bitcast(FP8X4), lhsT_scale=f_scale[g, q][:, texels],
+                rhs=light[g][:, side_cols(s)].bitcast(FP8X4), rhs_scale=light_scale[:, g, side_cols(s)],
                 start=(g == 0), stop=(g == 2),
             )
 
-        def tint_rows(k, half):
-            q, i = divmod(k, 2)
-            n = slice(512 * half, 512 * (half + 1))
-            lit[k, half] = work.tile([P, 512], F32, name="lit", bufs=8)
-            nc.vector.scalar_tensor_tensor(
-                out=lit[k, half][:], in0=accs[k, half][:], scalar=tint_sb[:, q, i : i + 1],
-                in1=bounce_sb[q][:, i, n], op0=ALU.mult, op1=ALU.add,
-            )
-
-        def stage2(k):
-            for half in range(2):
+        def stage2(rt):
+            for s in range(2):
                 for g in range(3):
-                    stage2_pass(k, half, g)
+                    stage2_pass(rt, s, g)
 
-        def finish_rows(k, half, engine=nc.gpsimd):
-            q, i = divmod(k, 2)
-            n = slice(512 * half, 512 * (half + 1))
-            y = work.tile([P, 512], F32, name="y", bufs=6)
-            engine.tensor_tensor(out=y[:], in0=lit[k, half][:], in1=power_sb[:, n], op=ALU.mult)
+        def add_bounce(rt, s):
+            q, i = divmod(rt, 2)
+            lit[rt, s] = work.tile([P, SPAN], F32, name="lit", bufs=8)
+            nc.vector.scalar_tensor_tensor(
+                out=lit[rt, s][:], in0=reflected[rt, s][:], scalar=tint_sb[:, q, i : i + 1],
+                in1=bounce_sb[q][:, i, side_cols(s)], op0=ALU.mult, op1=ALU.add,
+            )
+
+        def apply_power(rt, s, engine):
+            q, i = divmod(rt, 2)
+            y_rows[rt, s] = work.tile([P, SPAN], F32, name="y", bufs=6)
+            engine.tensor_tensor(out=y_rows[rt, s][:], in0=lit[rt, s][:], in1=power_sb[:, side_cols(s)], op=ALU.mult)
             nc.sync.dma_start(
-                out=out_0[256 * q : 256 * (q + 1), n].rearrange("(p i) n -> p i n", i=2)[:, i, :], in_=y[:]
+                out=out_0[QUARTER * q : QUARTER * (q + 1), side_cols(s)].rearrange("(p i) n -> p i n", i=2)[:, i, :],
+                in_=y_rows[rt, s][:],
             )
-            y_rows[k, half] = y
 
-        def sort_rows(k, half):
-            y = y_rows[k, half]
-            y_sorted[k, half] = work.tile([P, 512], BF16, name="y_sorted", bufs=8)
+        def epilogue(rt, engine):
+            for s in range(2):
+                add_bounce(rt, s)
+            for s in range(2):
+                apply_power(rt, s, engine)
+
+        def round_y(rt, s):
+            y_sorted[rt, s] = work.tile([P, SPAN], BF16, name="y_sorted", bufs=8)
             nc.scalar.copy(
-                out=y_sorted[k, half][:].rearrange("p (u j e) -> p u j e", u=2, e=2),
-                in_=y[:].rearrange("p (j u e) -> p u j e", u=2, e=2),
+                out=y_sorted[rt, s][:].rearrange("p (u j e) -> p u j e", u=2, e=2),
+                in_=y_rows[rt, s][:].rearrange("p (j u e) -> p u j e", u=2, e=2),
             )
 
-        def epilogue(k, engine):
-            tint_rows(k, 0)
-            tint_rows(k, 1)
-            finish_rows(k, 0, engine)
-            finish_rows(k, 1, engine)
+        def round_both(rt):
+            for s in range(2):
+                round_y(rt, s)
 
-        def sort_both(k):
-            sort_rows(k, 0)
-            sort_rows(k, 1)
-
-        def turn_y(q, g, copy=nc.scalar.copy):
+        def turn_y(q, s, copy):
             turned = bank([P, 2, 2, P])
             for i in range(2):
-                words = y_sorted[2 * q + i, g][:].bitcast(F32)
+                words = y_sorted[2 * q + i, s][:].bitcast(F32)
                 for u in range(2):
                     nc.tensor.transpose(turned[:, i, u, :], words[:, P * u : P * (u + 1)], ident[:])
-            y_grouped[q, g] = work.tile([P, 1024], BF16, name="y_grouped", bufs=4, align_bytes=64)
+            y_grouped[q, s] = work.tile([P, 4 * QUARTER], BF16, name="y_grouped", bufs=4, align_bytes=64)
             copy(
-                out=y_grouped[q, g][:].bitcast(F32).rearrange("p (r i u) -> p r i u", i=2, u=2),
-                in_=turned[:].rearrange("p i u r -> p r i u"),
+                out=y_grouped[q, s][:].bitcast(F32).rearrange("j (r i u) -> j r i u", i=2, u=2),
+                in_=turned[:].rearrange("j i u r -> j r i u"),
             )
 
-        def quantize_y(q):
-            m = slice(256 * q, 256 * (q + 1))
-            y_code = kept("y_code_%d" % q, [P, 2, 256], U32)
-            for g in range(2):
-                nc.vector.quantize_mx(
-                    out=y_code[:, g, :].bitcast(FP8X4), scales=y_scale[:, g, m], in_=y_grouped[q, g][:]
-                )
+        def quantize_y(q, s):
+            if s == 0:
+                y_code[q] = kept("y_code_%d" % q, [P, 2, QUARTER], U32)
+            nc.vector.quantize_mx(
+                out=y_code[q][:, s, :].bitcast(FP8X4),
+                scales=y_scale[4 * s : P, QUARTER * q : QUARTER * (q + 1)],
+                in_=y_grouped[q, s][:],
+            )
+
+        def store_codes(q, sides):
             nc.sync.dma_start(
-                out=out_1[:, :, m, :].rearrange("g p m t -> p g (m t)").bitcast(I32), in_=y_code[:].bitcast(I32)
+                out=out_1[sides, :, QUARTER * q : QUARTER * (q + 1), :].rearrange("s p m t -> p s (m t)").bitcast(I32),
+                in_=y_code[q][:, sides, :].bitcast(I32),
             )
 
-        def unit(g, h, slots=range(4)):
-            for t in slots:
-                for c in range(3):
-                    stage1_pass(g, h, t, c)
-                exponentiate(g, h, t)
-
-        def turn_pair(first, second):
-            turn_coef(*first)
-            turn_coef(*second)
-
-        def helped_unit(g, h):
-            for t in range(4):
-                unit(g, h, (t,))
-                if t:
-                    scale_rows(g, h, t - 1)
-            scale_rows(g, h, 3)
+        both_sides = slice(0, 2)
 
         turn_pair((0, 0), (0, 1))
         order_fine_codes(0)
@@ -346,15 +355,16 @@ def tile_log_brdf_environment_transport_k6_kernel(
         quantize_coef(0, 0)
         quantize_coef(0, 1)
         group_basis(0, 0, nc.vector.tensor_copy)
+        order_fine_scales(0)
         turn_pair((1, 0), (2, 0))
         turn_pair((1, 1), (2, 1))
         quantize_basis(0, 1)
         quantize_basis(0, 0)
         quantize_coef(1, 0)
         quantize_coef(2, 0)
-        order_fine_scales(0)
         quantize_coef(1, 1)
         quantize_coef(2, 1)
+
         group_basis(1, 0, nc.scalar.copy)
         group_basis(1, 1, nc.scalar.copy)
         order_fine_codes(1)
@@ -368,6 +378,7 @@ def tile_log_brdf_environment_transport_k6_kernel(
             for c in (1, 2):
                 stage1_pass(0, 0, t, c)
             exponentiate(0, 0, t)
+
         order_fine_scales(2)
         group_basis(2, 0, nc.vector.tensor_copy)
         turn_pair((0, 2), (0, 3))
@@ -393,68 +404,81 @@ def tile_log_brdf_environment_transport_k6_kernel(
         unit(2, 0)
         quantize_f(1, 0)
         quantize_f(1, 1)
+
         nc.scalar.copy(out=cos_f32[:], in_=cos_sb[:])
-        helped_unit(0, 1)
+        f_rows = unit_weighed_on_scalar(0, 1)
         make_f(2, 0)
         stage2(0)
         stage2(1)
         epilogue(0, nc.vector)
-        group_f(0, 2)
-        group_f(0, 3)
-        tint_rows(1, 0)
+        group_f(0, 2, f_rows)
+        group_f(0, 3, f_rows)
+        add_bounce(1, 0)
         quantize_f(0, 2)
         quantize_f(0, 3)
-        tint_rows(1, 1)
-        finish_rows(1, 0, nc.vector)
-        finish_rows(1, 1, nc.vector)
-        sort_both(0)
+        add_bounce(1, 1)
+        apply_power(1, 0, nc.vector)
+        apply_power(1, 1, nc.vector)
+        round_both(0)
         unit(1, 1)
-        sort_both(1)
+        round_both(1)
         stage2(2)
         make_f(1, 1)
         epilogue(2, nc.vector)
         unit(2, 1)
-        turn_y(0, 0)
-        turn_y(0, 1)
-        sort_both(2)
+        for s in range(2):
+            turn_y(0, s, nc.scalar.copy)
+        round_both(2)
+
         stage2(3)
-        for k in (4, 5):
-            for half in range(2):
+        for rt in (4, 5):
+            for s in range(2):
                 for g in range(2):
-                    stage2_pass(k, half, g)
-        make_f(2, 1)
-        quantize_y(0)
-        for k in (4, 5):
-            for half in range(2):
-                stage2_pass(k, half, 2)
+                    stage2_pass(rt, s, g)
+        weigh(2, 2)
+        weigh(2, 3)
+        for s in range(2):
+            quantize_f(2, 2 + s)
+            quantize_y(0, s)
+        store_codes(0, both_sides)
+        for rt in (4, 5):
+            for s in range(2):
+                stage2_pass(rt, s, 2)
+
         epilogue(3, nc.gpsimd)
-        sort_both(3)
+        round_both(3)
         epilogue(4, nc.gpsimd)
-        tint_rows(5, 0)
-        tint_rows(5, 1)
-        for half in range(2):
-            for k in (6, 7):
+        for s in range(2):
+            add_bounce(5, s)
+        for s in range(2):
+            for rt in (6, 7):
                 for g in range(3):
-                    stage2_pass(k, half, g)
-            turn_y(1, half)
-            sort_rows(4, half)
-        for half in range(2):
-            tint_rows(6, half)
-            tint_rows(7, half)
-        last = ((5, 0), (5, 1), (6, 0), (7, 0), (6, 1), (7, 1))
-        for k, half in last:
-            finish_rows(k, half, nc.vector)
-        for k, half in last:
-            sort_rows(k, half)
-        quantize_y(1)
-        turn_y(2, 0, nc.vector.tensor_copy)
-        turn_y(2, 1, nc.vector.tensor_copy)
-        turn_y(3, 0)
-        turn_y(3, 1)
-        quantize_y(2)
-        quantize_y(3)
-        for quad in range(4):
+                    stage2_pass(rt, s, g)
+            turn_y(1, s, nc.scalar.copy)
+            round_y(4, s)
+        for s in range(2):
+            for rt in (6, 7):
+                add_bounce(rt, s)
+        remaining = [(5, s) for s in range(2)] + [(rt, s) for s in range(2) for rt in (6, 7)]
+        for rt, s in remaining:
+            apply_power(rt, s, nc.vector)
+        for rt, s in remaining:
+            round_y(rt, s)
+        for s in range(2):
+            quantize_y(1, s)
+            turn_y(2, s, nc.vector.tensor_copy)
+        store_codes(1, both_sides)
+        for s in range(2):
+            turn_y(3, s, nc.scalar.copy)
+        quantize_y(2, 0)
+        quantize_y(3, 0)
+        store_codes(3, slice(0, 1))
+        quantize_y(2, 1)
+        store_codes(2, both_sides)
+        quantize_y(3, 1)
+        store_codes(3, slice(1, 2))
+        for n in range(4):
             nc.scalar.dma_start(
-                out=out_2[:, 4 * quad : 4 * quad + 4, :].rearrange("g r m -> r g m").bitcast(I32),
-                in_=y_scale[32 * quad : 32 * quad + 4, :, :].bitcast(I32),
+                out=out_2[:, 4 * n : 4 * n + 4, :].bitcast(I32),
+                in_=y_scale[32 * n : 32 * n + 8, :].bitcast(I32),
             )

from contextlib import ExitStack

import concourse.mybir as mybir
from concourse.masks import make_identity

TEXELS, LEAD, FINE, BINS, PATTERNS = 1024, 512, 1024, 1536, 1024
FLOPS = 2 * TEXELS * (LEAD + FINE) * BINS + 2 * TEXELS * BINS * PATTERNS

F32 = mybir.dt.float32
BF16 = mybir.dt.bfloat16
I32 = mybir.dt.int32
U32 = mybir.dt.uint32
U8 = mybir.dt.uint8
FP8X4 = mybir.dt.float8_e4m3fn_x4
FP4X4 = mybir.dt.float4_e2m1fn_x4
ACT = mybir.ActivationFunctionType
ALU = mybir.AluOpType

P = 128
SPAN = 512
QUARTER = 256


def tile_log_brdf_environment_transport_k6_kernel(
    tc, coef_lead, basis_lead, coef_fine, fine_words, fine_scales, cos_weight,
    light_words, light_scales, tint, bounce, power, out_0, out_1, out_2,
):
    nc = tc.nc
    with ExitStack() as ctx:
        keep = ctx.enter_context(tc.tile_pool(name="keep", bufs=1))
        work = ctx.enter_context(tc.tile_pool(name="work", bufs=1))
        psum = ctx.enter_context(tc.psum_pool(name="psum", bufs=1))
        ctx.enter_context(tc.manual_schedule())

        def kept(name, shape, dtype):
            return keep.tile(shape, dtype, name=name, align_bytes=64)

        def bank(shape):
            return psum.tile(shape, F32, name="bank", bufs=8)

        ident = kept("ident", [P, P], F32)
        warm = kept("warm", [P, 16], F32)
        first_scale_raw = kept("first_scale_raw", [P, 2, SPAN], U8)
        later_scale_raw = kept("later_scale_raw", [P, 2, BINS - SPAN], U8)
        light_scale = kept("light_scale", [P, 3, PATTERNS], U8)
        cos_sb = kept("cos_sb", [P, 3, 4], BF16)
        tint_sb = kept("tint_sb", [P, 4, 2], BF16)
        power_sb = kept("power_sb", [P, PATTERNS], BF16)
        y_scale = kept("y_scale", [P, TEXELS], U8)

        make_identity(nc, ident[:])
        nc.vector.memset(first_scale_raw[:].bitcast(I32), 0)
        nc.vector.memset(warm[:], 0.0)
        nc.vector.memset(later_scale_raw[:].bitcast(I32), 0)
        nc.vector.memset(light_scale[:].bitcast(I32), 0)
        nc.scalar.activation(out=warm[:, 8:9], in_=warm[:, 0:1], func=ACT.Exp)

        lead_raw, fine_coef_raw, basis_raw, fine_word_raw, light, bounce_sb = {}, {}, {}, {}, {}, {}

        def load_lead(h):
            lead_raw[h] = kept("lead_raw_%d" % h, [P, 2, 2 * LEAD], BF16)
            nc.sync.dma_start(
                out=lead_raw[h][:],
                in_=coef_lead[SPAN * h : SPAN * (h + 1), :].rearrange("(q p i) k -> p q (i k)", q=2, i=2),
            )

        def load_fine_coef(q):
            fine_coef_raw[q] = kept("fine_coef_raw_%d" % q, [P, 2 * FINE], BF16)
            nc.sync.dma_start(
                out=fine_coef_raw[q][:],
                in_=coef_fine[QUARTER * q : QUARTER * (q + 1), :].rearrange("(p i) k -> p (i k)", i=2),
            )

        def load_fine_words(g):
            fine_word_raw[g] = kept("fine_word_raw_%d" % g, [P, 2, 2 * SPAN], U8)
            nc.sync.dma_start(
                out=fine_word_raw[g][:].bitcast(I32),
                in_=fine_words[:, :, 2 * SPAN * g : 2 * SPAN * (g + 1)].rearrange("c p b -> p c b").bitcast(I32),
            )

        def load_basis(g):
            basis_raw[g] = kept("basis_raw_%d" % g, [P, 4, SPAN], BF16)
            nc.sync.dma_start(
                out=basis_raw[g][:],
                in_=basis_lead[:, SPAN * g : SPAN * (g + 1)].rearrange("(p j) d -> p j d", j=4),
            )

        def load_scale_rows(plane, rows):
            for n in range(4):
                nc.sync.dma_start(
                    out=plane[32 * n : 32 * n + 4, :, :].bitcast(I32),
                    in_=rows[:, 4 * n : 4 * n + 4, :].rearrange("c r d -> r c d").bitcast(I32),
                )

        load_lead(0)
        load_scale_rows(first_scale_raw, fine_scales[:, :, 0:SPAN])
        load_fine_words(0)
        load_basis(0)
        load_fine_coef(0)
        load_fine_coef(1)
        load_fine_words(1)
        load_basis(1)
        load_scale_rows(later_scale_raw, fine_scales[:, :, SPAN:BINS])
        load_fine_words(2)
        load_lead(1)
        load_basis(2)
        nc.sync.dma_start(out=cos_sb[:], in_=cos_weight.rearrange("(g p t) -> p g t", g=3, t=4))
        load_fine_coef(2)
        load_fine_coef(3)
        load_scale_rows(light_scale, light_scales)
        for g in range(3):
            light[g] = kept("light_%d" % g, [P, PATTERNS], U32)
            nc.sync.dma_start(
                out=light[g][:].bitcast(I32),
                in_=light_words[g].rearrange("p n t -> p (n t)").bitcast(I32),
            )
        nc.sync.dma_start(out=tint_sb[:], in_=tint.rearrange("(q p i) -> p q i", q=4, i=2))
        for q in range(4):
            bounce_sb[q] = kept("bounce_%d" % q, [P, 2, PATTERNS], BF16)
            nc.sync.dma_start(
                out=bounce_sb[q][:],
                in_=bounce[QUARTER * q : QUARTER * (q + 1), :].rearrange("(p i) n -> p i n", i=2),
            )
            if q == 0:
                nc.sync.dma_start(out=power_sb[:], in_=power.partition_broadcast(P))

        coef_grouped, coef_code, coef_scale = {}, {}, {}

        def turn_coef(c, q):
            turned = bank([P, 2, 2, P])
            for i in range(2):
                if c == 0:
                    words = lead_raw[q // 2][:, q % 2, :].bitcast(F32)[:, QUARTER * i : QUARTER * (i + 1)]
                else:
                    first = FINE // 2 * i + QUARTER * (c - 1)
                    words = fine_coef_raw[q][:].bitcast(F32)[:, first : first + QUARTER]
                for u in range(2):
                    nc.tensor.transpose(turned[:, i, u, :], words[:, u:QUARTER:2], ident[:])
            coef_grouped[c, q] = work.tile([P, 4 * QUARTER], BF16, name="coef_grouped", bufs=6, align_bytes=64)
            nc.scalar.copy(
                out=coef_grouped[c, q][:].bitcast(F32).rearrange("p (i r u) -> p i r u", i=2, u=2),
                in_=turned[:].rearrange("p i u r -> p i r u"),
            )

        def turn_pair(first, second):
            turn_coef(*first)
            turn_coef(*second)

        def quantize_coef(c, q):
            h = q // 2
            if q % 2 == 0:
                coef_code[c, h] = kept("coef_code_%d_%d" % (c, h), [P, SPAN], U32)
                coef_scale[c, h] = kept("coef_scale_%d_%d" % (c, h), [P, SPAN], U8)
            cols = slice(QUARTER * (q % 2), QUARTER * (q % 2 + 1))
            nc.vector.quantize_mx(
                out=coef_code[c, h][:, cols].bitcast(FP8X4),
                scales=coef_scale[c, h][:, cols],
                in_=coef_grouped[c, q][:],
            )

        fine_code, fine_scale, basis_grouped, basis_code, basis_scale = {}, {}, {}, {}, {}

        def order_fine_codes(g):
            fine_code[g] = kept("fine_code_%d" % g, [P, 4, 2, 2 * P], U8)
            nc.vector.tensor_copy(
                out=fine_code[g][:].rearrange("p t c (a m b) -> p (c a) t m b", m=8, b=2),
                in_=fine_word_raw[g][:].rearrange("p c (a m t b) -> p (c a) t m b", m=8, t=4, b=2),
            )

        def order_fine_scales(g):
            raw = first_scale_raw[:] if g == 0 else later_scale_raw[:, :, SPAN * (g - 1) : SPAN * g]
            fine_scale[g] = kept("fine_scale_%d" % g, [P, 4, 2, P], U8)
            nc.vector.tensor_copy(
                out=fine_scale[g][:].rearrange("p t c (a m) -> p c a t m", m=16),
                in_=raw.rearrange("p c (a m t) -> p c a t m", m=16, t=4),
            )

        def group_basis(g, pair, copy):
            basis_grouped[g, pair] = work.tile([P, 2, P, 4], BF16, name="basis_grouped", bufs=3, align_bytes=64)
            copy(
                out=basis_grouped[g, pair][:].rearrange("p t (a m) j -> p a t m j", m=2),
                in_=basis_raw[g][:].rearrange("p j (a m t) -> p a t m j", m=2, t=4)[:, :, 2 * pair : 2 * pair + 2],
            )

        def quantize_basis(g, pair):
            basis_code[g, pair] = kept("basis_code_%d_%d" % (g, pair), [P, 2 * P], U32)
            basis_scale[g, pair] = kept("basis_scale_%d_%d" % (g, pair), [P, 2 * P], U8)
            nc.vector.quantize_mx(
                out=basis_code[g, pair][:].bitcast(FP8X4),
                scales=basis_scale[g, pair][:],
                in_=basis_grouped[g, pair][:].rearrange("p t m j -> p (t m j)"),
            )

        log_brdf, brdf, f_grouped, f_code, f_scale = {}, {}, {}, {}, {}

        def stage1_pass(g, h, t, c):
            if c == 0:
                log_brdf[g, h, t] = bank([P, SPAN])
                weights = basis_code[g, t // 2][:, P * (t % 2) : P * (t % 2 + 1)].bitcast(FP8X4)
                scales = basis_scale[g, t // 2][:, P * (t % 2) : P * (t % 2 + 1)]
            else:
                weights = fine_code[g][:, t, c - 1, :].bitcast(FP4X4)
                scales = fine_scale[g][:, t, c - 1, :]
            nc.tensor.matmul_mx(
                out=log_brdf[g, h, t][:], lhsT=weights, lhsT_scale=scales,
                rhs=coef_code[c, h][:].bitcast(FP8X4), rhs_scale=coef_scale[c, h][:],
                start=(c == 0), stop=(c == 2),
            )

        def exponentiate(g, h, t):
            if t == 0:
                brdf[g, h] = work.tile([P, 4, SPAN], F32, name="brdf", bufs=3)
            nc.scalar.activation(out=brdf[g, h][:, t, :], in_=log_brdf[g, h, t][:], func=ACT.Exp)

        def unit(g, h, slots=range(4)):
            for t in slots:
                for c in range(3):
                    stage1_pass(g, h, t, c)
                exponentiate(g, h, t)

        def quarter_cols(q):
            return slice(QUARTER * (q % 2), QUARTER * (q % 2 + 1))

        def new_f_grouped(g, q):
            f_grouped[g, q] = work.tile([P, 4 * QUARTER], BF16, name="f_grouped", bufs=4, align_bytes=64)
            return f_grouped[g, q][:].rearrange("p (a r t) -> p a t r", r=4, t=4)

        def weigh(g, q):
            nc.vector.tensor_tensor(
                out=new_f_grouped(g, q),
                in0=brdf[g, q // 2][:, :, quarter_cols(q)].rearrange("p t (a r) -> p a t r", r=4),
                in1=cos_sb[:, g, :].rearrange("p (a t r) -> p a t r", a=1, r=1).to_broadcast([P, QUARTER // 4, 4, 4]),
                op=ALU.mult,
            )

        cos_f32 = kept("cos_f32", [P, 3, 4], F32)

        def unit_weighed_on_scalar(g, h):
            unit(g, h, (0, 1))
            rows = work.tile([P, 4, SPAN], BF16, name="f_rows", bufs=1)
            for t in range(4):
                nc.scalar.activation(
                    out=rows[:, t, :], in_=brdf[g, h][:, t, :], func=ACT.Copy, scale=cos_f32[:, g, t : t + 1]
                )
                if t + 2 < 4:
                    unit(g, h, (t + 2,))
            return rows

        def group_f(g, q, rows):
            nc.vector.tensor_copy(
                out=new_f_grouped(g, q), in_=rows[:, :, quarter_cols(q)].rearrange("p t (a r) -> p a t r", r=4)
            )

        def quantize_f(g, q):
            f_code[g, q] = kept("f_code_%d_%d" % (g, q), [P, QUARTER], U32)
            f_scale[g, q] = kept("f_scale_%d_%d" % (g, q), [P, QUARTER], U8)
            nc.vector.quantize_mx(
                out=f_code[g, q][:].bitcast(FP8X4), scales=f_scale[g, q][:], in_=f_grouped[g, q][:]
            )

        def make_f(g, h):
            for q in (2 * h, 2 * h + 1):
                weigh(g, q)
            for q in (2 * h, 2 * h + 1):
                quantize_f(g, q)

        reflected, lit, y_rows, y_sorted, y_grouped, y_code = {}, {}, {}, {}, {}, {}

        def side_cols(s):
            return slice(SPAN * s, SPAN * (s + 1))

        def stage2_pass(rt, s, g):
            q, i = divmod(rt, 2)
            texels = slice(P * i, P * (i + 1))
            if g == 0:
                reflected[rt, s] = bank([P, SPAN])
            nc.tensor.matmul_mx(
                out=reflected[rt, s][:],
                lhsT=f_code[g, q][:, texels].bitcast(FP8X4), lhsT_scale=f_scale[g, q][:, texels],
                rhs=light[g][:, side_cols(s)].bitcast(FP8X4), rhs_scale=light_scale[:, g, side_cols(s)],
                start=(g == 0), stop=(g == 2),
            )

        def stage2(rt):
            for s in range(2):
                for g in range(3):
                    stage2_pass(rt, s, g)

        def add_bounce(rt, s):
            q, i = divmod(rt, 2)
            lit[rt, s] = work.tile([P, SPAN], F32, name="lit", bufs=8)
            nc.vector.scalar_tensor_tensor(
                out=lit[rt, s][:], in0=reflected[rt, s][:], scalar=tint_sb[:, q, i : i + 1],
                in1=bounce_sb[q][:, i, side_cols(s)], op0=ALU.mult, op1=ALU.add,
            )

        def apply_power(rt, s, engine):
            q, i = divmod(rt, 2)
            y_rows[rt, s] = work.tile([P, SPAN], F32, name="y", bufs=6)
            engine.tensor_tensor(out=y_rows[rt, s][:], in0=lit[rt, s][:], in1=power_sb[:, side_cols(s)], op=ALU.mult)
            nc.sync.dma_start(
                out=out_0[QUARTER * q : QUARTER * (q + 1), side_cols(s)].rearrange("(p i) n -> p i n", i=2)[:, i, :],
                in_=y_rows[rt, s][:],
            )

        def epilogue(rt, engine):
            for s in range(2):
                add_bounce(rt, s)
            for s in range(2):
                apply_power(rt, s, engine)

        def round_y(rt, s):
            y_sorted[rt, s] = work.tile([P, SPAN], BF16, name="y_sorted", bufs=8)
            nc.scalar.copy(
                out=y_sorted[rt, s][:].rearrange("p (u j e) -> p u j e", u=2, e=2),
                in_=y_rows[rt, s][:].rearrange("p (j u e) -> p u j e", u=2, e=2),
            )

        def round_both(rt):
            for s in range(2):
                round_y(rt, s)

        def turn_y(q, s, copy):
            turned = bank([P, 2, 2, P])
            for i in range(2):
                words = y_sorted[2 * q + i, s][:].bitcast(F32)
                for u in range(2):
                    nc.tensor.transpose(turned[:, i, u, :], words[:, P * u : P * (u + 1)], ident[:])
            y_grouped[q, s] = work.tile([P, 4 * QUARTER], BF16, name="y_grouped", bufs=4, align_bytes=64)
            copy(
                out=y_grouped[q, s][:].bitcast(F32).rearrange("j (r i u) -> j r i u", i=2, u=2),
                in_=turned[:].rearrange("j i u r -> j r i u"),
            )

        def quantize_y(q, s):
            if s == 0:
                y_code[q] = kept("y_code_%d" % q, [P, 2, QUARTER], U32)
            nc.vector.quantize_mx(
                out=y_code[q][:, s, :].bitcast(FP8X4),
                scales=y_scale[4 * s : P, QUARTER * q : QUARTER * (q + 1)],
                in_=y_grouped[q, s][:],
            )

        def store_codes(q, sides):
            nc.sync.dma_start(
                out=out_1[sides, :, QUARTER * q : QUARTER * (q + 1), :].rearrange("s p m t -> p s (m t)").bitcast(I32),
                in_=y_code[q][:, sides, :].bitcast(I32),
            )

        both_sides = slice(0, 2)

        turn_pair((0, 0), (0, 1))
        order_fine_codes(0)
        group_basis(0, 1, nc.scalar.copy)
        quantize_coef(0, 0)
        quantize_coef(0, 1)
        group_basis(0, 0, nc.vector.tensor_copy)
        order_fine_scales(0)
        turn_pair((1, 0), (2, 0))
        turn_pair((1, 1), (2, 1))
        quantize_basis(0, 1)
        quantize_basis(0, 0)
        quantize_coef(1, 0)
        quantize_coef(2, 0)
        quantize_coef(1, 1)
        quantize_coef(2, 1)

        group_basis(1, 0, nc.scalar.copy)
        group_basis(1, 1, nc.scalar.copy)
        order_fine_codes(1)
        order_fine_scales(1)
        order_fine_codes(2)
        quantize_basis(1, 0)
        quantize_basis(1, 1)
        for t in range(4):
            stage1_pass(0, 0, t, 0)
        for t in range(4):
            for c in (1, 2):
                stage1_pass(0, 0, t, c)
            exponentiate(0, 0, t)

        order_fine_scales(2)
        group_basis(2, 0, nc.vector.tensor_copy)
        turn_pair((0, 2), (0, 3))
        unit(1, 0, (0, 1))
        group_basis(2, 1, nc.scalar.copy)
        turn_pair((1, 2), (2, 2))
        unit(1, 0, (2, 3))
        turn_pair((1, 3), (2, 3))
        weigh(0, 0)
        quantize_basis(2, 0)
        weigh(0, 1)
        quantize_f(0, 0)
        quantize_basis(2, 1)
        quantize_f(0, 1)
        quantize_coef(0, 2)
        quantize_coef(0, 3)
        quantize_coef(1, 2)
        quantize_coef(2, 2)
        weigh(1, 0)
        weigh(1, 1)
        quantize_coef(1, 3)
        quantize_coef(2, 3)
        unit(2, 0)
        quantize_f(1, 0)
        quantize_f(1, 1)

        nc.scalar.copy(out=cos_f32[:], in_=cos_sb[:])
        f_rows = unit_weighed_on_scalar(0, 1)
        make_f(2, 0)
        stage2(0)
        stage2(1)
        epilogue(0, nc.vector)
        group_f(0, 2, f_rows)
        group_f(0, 3, f_rows)
        add_bounce(1, 0)
        quantize_f(0, 2)
        quantize_f(0, 3)
        add_bounce(1, 1)
        apply_power(1, 0, nc.vector)
        apply_power(1, 1, nc.vector)
        round_both(0)
        unit(1, 1)
        round_both(1)
        stage2(2)
        make_f(1, 1)
        epilogue(2, nc.vector)
        unit(2, 1)
        for s in range(2):
            turn_y(0, s, nc.scalar.copy)
        round_both(2)

        stage2(3)
        for rt in (4, 5):
            for s in range(2):
                for g in range(2):
                    stage2_pass(rt, s, g)
        weigh(2, 2)
        weigh(2, 3)
        for s in range(2):
            quantize_f(2, 2 + s)
            quantize_y(0, s)
        store_codes(0, both_sides)
        for rt in (4, 5):
            for s in range(2):
                stage2_pass(rt, s, 2)

        epilogue(3, nc.gpsimd)
        round_both(3)
        epilogue(4, nc.gpsimd)
        for s in range(2):
            add_bounce(5, s)
        for s in range(2):
            for rt in (6, 7):
                for g in range(3):
                    stage2_pass(rt, s, g)
            turn_y(1, s, nc.scalar.copy)
            round_y(4, s)
        for s in range(2):
            for rt in (6, 7):
                add_bounce(rt, s)
        remaining = [(5, s) for s in range(2)] + [(rt, s) for s in range(2) for rt in (6, 7)]
        for rt, s in remaining:
            apply_power(rt, s, nc.vector)
        for rt, s in remaining:
            round_y(rt, s)
        for s in range(2):
            quantize_y(1, s)
            turn_y(2, s, nc.vector.tensor_copy)
        store_codes(1, both_sides)
        for s in range(2):
            turn_y(3, s, nc.scalar.copy)
        quantize_y(2, 0)
        quantize_y(3, 0)
        store_codes(3, slice(0, 1))
        quantize_y(2, 1)
        store_codes(2, both_sides)
        quantize_y(3, 1)
        store_codes(3, slice(1, 2))
        for n in range(4):
            nc.scalar.dma_start(
                out=out_2[:, 4 * n : 4 * n + 4, :].bitcast(I32),
                in_=y_scale[32 * n : 32 * n + 8, :].bitcast(I32),
            )
